import numpy as np
import ml_dtypes


def mxq(x, axis, fmt="e4m3"):
    dtype, down = {"e4m3": (ml_dtypes.float8_e4m3fn, 7), "e5m2": (ml_dtypes.float8_e5m2, 14)}[fmt]
    v = np.moveaxis(np.asarray(x, np.float32).astype(ml_dtypes.bfloat16).astype(np.float64), axis, -1)
    blocks = v.reshape(v.shape[:-1] + (-1, 32))
    amax = np.abs(blocks).max(-1, keepdims=True)
    byte = np.maximum(np.where(amax > 0, np.frexp(amax)[1] - 1 + 127, 0) - down, 1)
    scale = np.exp2(byte - 127.0)
    codes = (blocks / scale).astype(np.float32).astype(dtype).astype(np.float64)
    return np.moveaxis((codes * scale).reshape(v.shape), -1, axis)


WIDE = False


def mx_kscale(k):
    if not WIDE:
        return np.ones(k)
    levels = np.array([10, -10, 5, -5, 0])
    if k % 512:
        return np.exp2(np.random.permutation(np.resize(levels, k // 32))).repeat(32)
    a = np.empty((k // 512, 16))
    for p in range(k // 512):
        a[p, :8] = np.random.permutation(np.resize(levels, 8))
        for g in range(8):
            far = levels[np.abs(levels - a[p, g]) >= 10]
            a[p, g + 8] = far[np.random.randint(len(far))]
    return np.exp2(a.ravel()).repeat(32)


BF16 = ml_dtypes.bfloat16


def bf(x):
    return np.asarray(x, np.float32).astype(BF16)


def f64(x):
    return np.asarray(x).astype(np.float64)


B, S, R, D, E, T = 16, 512, 256, 512, 256, 2


def draw0():
    s, t = mx_kscale(S), mx_kscale(D)
    return {
        "x": bf(np.random.standard_normal((B, S, D)) * s[:, None]),
        "mp": bf(np.random.standard_normal((R, S)) / np.sqrt(S) / s[None, :]),
        "mq": bf(np.random.standard_normal((R, S)) / np.sqrt(S) / s[None, :]),
        "mr": bf(np.random.standard_normal((R, S)) / np.sqrt(S) / s[None, :]),
        "coef": bf(np.random.uniform(0.4, 1.0, (T, D))),
        "gain": bf((1.0 + 0.1 * np.random.standard_normal(D)) * t),
        "wo": bf(np.random.standard_normal((D, E)) / np.sqrt(D) / t[:, None]),
    }


def mix_time(m, xq):
    return mxq(f64(m), 1, "e4m3") @ xq


def core(x, mp, mq, mr, coef, gain, wo):
    c = f64(coef)
    xq = mxq(f64(x), 1, "e4m3")
    p = mix_time(mp, xq)
    q = mix_time(mq, xq)
    r = mix_time(mr, xq)
    h = c[0] + c[1] * r
    y = p * (1.0 + q * h)
    z = y * f64(gain)
    return mxq(z, 2, "e4m3") @ mxq(f64(wo), 0, "e4m3")


def e4m3fn_bytes(y):
    return np.clip(np.asarray(y, np.float64), -448.0, 448.0).astype(np.float32).astype(ml_dtypes.float8_e4m3fn).view(np.uint8)


def e4m3fn_values(b):
    return np.asarray(b, np.uint8).view(ml_dtypes.float8_e4m3fn).astype(np.float64)


def setup_inputs():
    d = draw0()
    x0 = np.asarray(d['x']).astype(np.float64)
    s = (np.max(np.abs(x0), axis=(0, 2), keepdims=True) / 448.0).astype(np.float32)
    out = {}
    for k, v in d.items():
        if k == 'x':
            out['x_bytes'] = e4m3fn_bytes(x0 / s.astype(np.float64))
            out['x_scale'] = s
        else:
            out[k] = v
    return out


def reference(x_bytes, x_scale, mp, mq, mr, coef, gain, wo):
    return core(e4m3fn_values(x_bytes) * x_scale.astype(np.float64), mp, mq, mr, coef, gain, wo)

@@ -1,0 +1,329 @@
+from contextlib import ExitStack
+
+import concourse.mybir as mybir
+from concourse.masks import make_identity
+
+NB, S, D, T, E = 16, 512, 512, 256, 256
+P = 128
+FLOPS = NB * (2 * 3 * T * S * D + 2 * T * D * E)
+
+F32 = mybir.dt.float32
+BF16 = mybir.dt.bfloat16
+U32 = mybir.dt.uint32
+U8 = mybir.dt.uint8
+FP8 = mybir.dt.float8_e4m3fn
+X4 = mybir.dt.float8_e4m3fn_x4
+COPY = mybir.ActivationFunctionType.Copy
+IDENT = mybir.ActivationFunctionType.Identity
+ADD = mybir.AluOpType.add
+MULT = mybir.AluOpType.mult
+
+GROUPS = [[0]] + [[b, b + 1] for b in range(1, 15, 2)] + [[15]]
+
+
+def tile_volterrathirdordermixer_t_kernel(tc, x_bytes, x_scale, mp, mq, mr, coef, gain, wo, out):
+    nc = tc.nc
+    with ExitStack() as ctx:
+        const = ctx.enter_context(tc.tile_pool(name="const", bufs=1))
+        xbp = ctx.enter_context(tc.tile_pool(name="xbp", bufs=NB))
+        xsp = ctx.enter_context(tc.tile_pool(name="xsp", bufs=6))
+        xgp = ctx.enter_context(tc.tile_pool(name="xgp", bufs=3))
+        xcp = ctx.enter_context(tc.tile_pool(name="xcp", bufs=5))
+        work = ctx.enter_context(tc.tile_pool(name="work", bufs=3))
+        zp = ctx.enter_context(tc.tile_pool(name="zp", bufs=2))
+        zcp = ctx.enter_context(tc.tile_pool(name="zcp", bufs=3))
+        op = ctx.enter_context(tc.tile_pool(name="op", bufs=4))
+        psum = ctx.enter_context(tc.psum_pool(name="psum", bufs=2))
+        ctx.enter_context(tc.manual_schedule())
+
+        xb = {}
+
+        def load_x(b):
+            x_codes = xbp.tile([P, 4 * D], U8, name="x_codes", align_bytes=64)
+            nc.sync.dma_start(out=x_codes[:], in_=x_bytes[b].rearrange("(p t) d -> p (t d)", t=4))
+            xb[b] = x_codes
+
+        sc = const.tile([P, 4], F32, name="sc", align_bytes=64)
+        load_x(0)
+        nc.sync.dma_start(out=sc[:], in_=x_scale.rearrange("o (p t) z -> p (o t z)", t=4))
+        m_raw = []
+        for i, m in enumerate((mr, mq, mp)):
+            m_sb = const.tile([P, 2, S], BF16, name="m_sb%d" % i, align_bytes=64)
+            nc.sync.dma_start(out=m_sb[:], in_=m.rearrange("(p c) k -> p c k", c=2))
+            m_raw.append(m_sb)
+        load_x(1)
+        load_x(2)
+
+        rows = const.tile([P, P], BF16, name="rows", align_bytes=64)
+        warm = const.tile([P, 1], F32, name="warm")
+        nc.vector.memset(warm[:], 0.0)
+        nc.vector.memset(rows[:], 0.0)
+        nc.scalar.activation(out=warm[:], in_=warm[:], func=IDENT)
+        for v, vec in enumerate((coef[0], coef[1], gain)):
+            nc.scalar.dma_start(
+                out=rows[4 * v : 4 * v + 4, :].rearrange("p (g i) -> p g i", i=8),
+                in_=vec.rearrange("(g j i) -> j g i", j=4, i=8),
+            )
+        ident = const.tile([P, P], F32, name="ident", align_bytes=64)
+        make_identity(nc, ident[:])
+        ident_b = const.tile([P, P], BF16, name="ident_b", align_bytes=64)
+
+        w_raw = const.tile([P, 4, E], BF16, name="w_raw", align_bytes=64)
+        for g in range(16):
+            nc.sync.dma_start(
+                out=w_raw[8 * g : 8 * g + 8, :, :],
+                in_=wo[32 * g : 32 * g + 32, :].rearrange("(j i) e -> i j e", i=8),
+            )
+        for b in range(3, NB):
+            load_x(b)
+
+        xs, xg, xc, xsc = {}, {}, {}, {}
+
+        def widen(b, t, engine):
+            if b not in xs:
+                x_wide = xsp.tile([P, 4, D], BF16, name="x_wide", align_bytes=64)
+                xs[b] = x_wide
+            src = xb[b][:, t * D : (t + 1) * D].bitcast(FP8)
+            if engine == "S":
+                nc.scalar.activation(out=xs[b][:, t, :], in_=src, func=COPY, scale=sc[:, t : t + 1])
+            else:
+                nc.vector.tensor_scalar(
+                    out=xs[b][:, t, :], in0=src, scalar1=sc[:, t : t + 1], scalar2=None, op0=MULT
+                )
+
+        def xint(b):
+            x_il = xgp.tile([P, 4 * D], BF16, name="x_il", align_bytes=64)
+            xg[b] = x_il
+            nc.vector.tensor_copy(
+                out=x_il[:].rearrange("p (j g i t) -> p g j i t", j=4, g=16, i=8, t=4),
+                in_=xs[b][:].rearrange("p t (g j i) -> p g j i t", g=16, j=4, i=8),
+            )
+
+        def xq(b):
+            x_q = xcp.tile([P, D], U32, name="x_q", align_bytes=64)
+            x_qs = xcp.tile([P, D], U8, name="x_qs", align_bytes=64)
+            nc.vector.quantize_mx(out=x_q[:].bitcast(X4), scales=x_qs[:], in_=xg[b][:])
+            xc[b], xsc[b] = x_q, x_qs
+
+        mc, msc = [], []
+        m_il = []
+
+        def m_turn(i):
+            m_ps = psum.tile([P, 2, 2, P], F32, name="m_ps", tag="RQP"[i])
+            words = m_raw[i]
+            for c in range(2):
+                wv = words[:, c, :].bitcast(F32)
+                for u in range(2):
+                    nc.tensor.transpose(m_ps[:, c, u, :], wv[:, u : S // 2 : 2], ident[:])
+            m_g = const.tile([P, T, 4], BF16, name="m_g%d" % i, align_bytes=64)
+            dst = m_g[:].rearrange("p n t -> p (n t)").bitcast(F32).rearrange("p (c r u) -> p c r u", c=2, u=2)
+            nc.scalar.copy(out=dst, in_=m_ps[:].rearrange("p c u r -> p c r u"))
+            m_il.append(m_g)
+
+        def m_quant(i):
+            m_q = const.tile([P, T], U32, name="m_q%d" % i, align_bytes=64)
+            m_s = const.tile([P, T], U8, name="m_s%d" % i, align_bytes=64)
+            nc.vector.quantize_mx(
+                out=m_q[:].bitcast(X4), scales=m_s[:], in_=m_il[i][:].rearrange("p n t -> p (n t)")
+            )
+            mc.append(m_q)
+            msc.append(m_s)
+
+        R, Q, PP, H = {}, {}, {}, {}
+        zr = {}
+
+        def mm(n):
+            gi, j = units[n]
+            bs = GROUPS[gi]
+            w = len(bs) * T
+            r_ps = psum.tile([P, w], F32, name="r_ps", tag="R")
+            q_ps = psum.tile([P, w], F32, name="q_ps", tag="Q")
+            p_ps = psum.tile([P, w], F32, name="p_ps", tag="P")
+            for i, ps in enumerate((r_ps, q_ps, p_ps)):
+                for k, b in enumerate(bs):
+                    nc.tensor.matmul_mx(
+                        out=ps[:, k * T : (k + 1) * T],
+                        lhsT=xc[b][:, j * P : (j + 1) * P].bitcast(X4),
+                        lhsT_scale=xsc[b][:, j * P : (j + 1) * P],
+                        rhs=mc[i][:].bitcast(X4),
+                        rhs_scale=msc[i][:],
+                        start=True,
+                        stop=True,
+                    )
+            R[n], Q[n], PP[n] = r_ps, q_ps, p_ps
+
+        def h_of(n):
+            gi, j = units[n]
+            w = len(GROUPS[gi]) * T
+            h_sb = work.tile([P, w], F32, name="h_sb", align_bytes=64)
+            nc.scalar.activation(
+                out=h_sb[:], in_=R[n][:], func=IDENT, bias=gc[:, j : j + 1], scale=gc[:, 4 + j : 5 + j]
+            )
+            H[n] = h_sb
+
+        U = {}
+
+        def first(n):
+            gi, j = units[n]
+            w = len(GROUPS[gi]) * T
+            u_sb = work.tile([P, w], F32, name="u_sb", align_bytes=64)
+            nc.vector.tensor_tensor(out=u_sb[:], in0=H[n][:], in1=Q[n][:], op=MULT)
+            U[n] = u_sb
+
+        def second(n):
+            gi, j = units[n]
+            w = len(GROUPS[gi]) * T
+            if j == 0:
+                z_raw = zp.tile([P, 4, w], BF16, name="z_raw", align_bytes=64)
+                zr[gi] = z_raw
+            nc.vector.scalar_tensor_tensor(
+                out=zr[gi][:, j, :], in0=U[n][:], scalar=cf[:, 8 + j : 9 + j], in1=PP[n][:], op0=ADD, op1=MULT
+            )
+
+        zil, zc, zsc = {}, {}, {}
+
+        def zint(gi, k):
+            z_il = zcp.tile([P, T, 4], BF16, name="z_il", align_bytes=64)
+            nc.vector.tensor_copy(
+                out=z_il[:], in_=zr[gi][:, :, k * T : (k + 1) * T].rearrange("p j t -> p t j")
+            )
+            zil[gi, k] = z_il
+
+        def zq(gi, k):
+            z_q = zcp.tile([P, T], U32, name="z_q", align_bytes=64)
+            z_s = zcp.tile([P, T], U8, name="z_s", align_bytes=64)
+            nc.vector.quantize_mx(
+                out=z_q[:].bitcast(X4), scales=z_s[:], in_=zil[gi, k][:].rearrange("p t j -> p (t j)")
+            )
+            zc[gi, k], zsc[gi, k] = z_q, z_s
+
+        O = {}
+
+        def omm(gi, k):
+            o_ps = psum.tile([P, 2, E], F32, name="o_ps", tag="O")
+            for c in range(2):
+                nc.tensor.matmul_mx(
+                    out=o_ps[:, c, :],
+                    lhsT=zc[gi, k][:, c * P : (c + 1) * P].bitcast(X4),
+                    lhsT_scale=zsc[gi, k][:, c * P : (c + 1) * P],
+                    rhs=w_q[:].bitcast(X4),
+                    rhs_scale=w_s[:],
+                    start=True,
+                    stop=True,
+                )
+            O[gi, k] = o_ps
+
+        def ocopy(gi, k):
+            o_sb = op.tile([P, 2, E], F32, name="o_sb", align_bytes=64)
+            nc.scalar.copy(out=o_sb[:], in_=O[gi, k][:])
+            nc.sync.dma_start(out=out[GROUPS[gi][k]].rearrange("(p c) e -> p c e", c=2), in_=o_sb[:])
+
+        widen(0, 2, "V")
+        widen(0, 3, "V")
+        widen(0, 0, "S")
+        widen(0, 1, "S")
+        m_turn(0)
+        xint(0)
+        m_turn(1)
+        nc.vector.tensor_copy(out=ident_b[:], in_=ident[:])
+        c_ps = psum.tile([P, P], BF16, name="c_ps", tag="O")
+        nc.tensor.transpose(c_ps[:], rows[:], ident_b[:])
+        cf = const.tile([P, 12], F32, name="cf", align_bytes=64)
+        nc.vector.tensor_copy(out=cf[:], in_=c_ps[:, 0:12])
+        m_quant(0)
+        xq(0)
+        gc = const.tile([P, 8], F32, name="gc", align_bytes=64)
+        nc.vector.tensor_tensor(out=gc[:, 0:4], in0=cf[:, 0:4], in1=cf[:, 8:12], op=MULT)
+        nc.vector.tensor_tensor(out=gc[:, 4:8], in0=cf[:, 4:8], in1=cf[:, 8:12], op=MULT)
+        m_turn(2)
+        m_quant(1)
+        m_quant(2)
+        widen(1, 2, "V")
+        widen(1, 3, "V")
+
+        units = [(gi, j) for gi in range(len(GROUPS)) for j in range(4)]
+        last = len(GROUPS) - 1
+        total = len(units)
+        mm(0)
+        h_of(0)
+        w_il = const.tile([P, E, 4], BF16, name="w_il", align_bytes=64)
+        w_q = const.tile([P, E], U32, name="w_q", align_bytes=64)
+        w_s = const.tile([P, E], U8, name="w_s", align_bytes=64)
+        widen(1, 0, "S")
+        widen(1, 1, "S")
+        mm(1)
+        h_of(1)
+        first(0)
+        for n, (gi, j) in enumerate(units):
+            if n + 1 < total:
+                first(n + 1)
+            second(n)
+            nxt = GROUPS[gi + 1] if gi + 1 <= last else []
+            nn = GROUPS[gi + 2] if gi + 2 <= last else []
+            prev = GROUPS[gi - 1] if gi > 0 else []
+            if gi == 0:
+                if j == 0:
+                    xint(1)
+                elif j == 1:
+                    xq(1)
+                    xint(2)
+                elif j == 2:
+                    xq(2)
+                else:
+                    nc.vector.tensor_copy(out=w_il[:], in_=w_raw[:].rearrange("p j e -> p e j"))
+                    xint(3)
+            elif nxt:
+                if j == 0:
+                    xq(nxt[0])
+                    if len(nxt) > 1:
+                        xint(nxt[1])
+                elif j == 1:
+                    if len(nxt) > 1:
+                        xq(nxt[1])
+                    if gi == 1:
+                        nc.vector.quantize_mx(
+                            out=w_q[:].bitcast(X4), scales=w_s[:], in_=w_il[:].rearrange("p e j -> p (e j)")
+                        )
+                    zint(gi - 1, 0)
+                elif j == 2:
+                    if len(prev) > 1:
+                        zint(gi - 1, 1)
+                        zq(gi - 1, 0)
+                else:
+                    if nn:
+                        xint(nn[0])
+                    if len(prev) > 1:
+                        zq(gi - 1, 1)
+                    else:
+                        zq(gi - 1, 0)
+            else:
+                if j == 0:
+                    zint(gi - 1, 0)
+                elif j == 1:
+                    zint(gi - 1, 1)
+                    zq(gi - 1, 0)
+                elif j == 2:
+                    zq(gi - 1, 1)
+            if n + 2 < total:
+                mm(n + 2)
+                h_of(n + 2)
+            if j == 0 and gi >= 2:
+                ocopy(gi - 2, len(GROUPS[gi - 2]) - 1)
+            if j == 2 and len(prev) > 1:
+                omm(gi - 1, 0)
+            if j == 3 and prev:
+                if len(prev) > 1:
+                    ocopy(gi - 1, 0)
+                omm(gi - 1, len(prev) - 1)
+            if gi == 0:
+                todo = [[(2, t) for t in range(4)], [(3, 0), (3, 1)], [(3, 2), (3, 3)], [(4, t) for t in range(4)]][j]
+            else:
+                ahead = [(b, t) for b in nn for t in range(4)]
+                todo = ahead[2 * j : 2 * j + 2]
+            for b, t in todo:
+                widen(b, t, "S")
+        zint(last, 0)
+        ocopy(last - 1, 1)
+        zq(last, 0)
+        omm(last, 0)
+        ocopy(last, 0)

@@ -18,7 +18,7 @@ IDENT = mybir.ActivationFunctionType.Identity
 ADD = mybir.AluOpType.add
 MULT = mybir.AluOpType.mult
 
-GROUPS = [[0]] + [[b, b + 1] for b in range(1, 15, 2)] + [[15]]
+GROUPS = [[0], [1]] + [[b, b + 1] for b in range(2, 14, 2)] + [[14], [15]]
 
 
 def tile_volterrathirdordermixer_t_kernel(tc, x_bytes, x_scale, mp, mq, mr, coef, gain, wo, out):
@@ -30,8 +30,8 @@ def tile_volterrathirdordermixer_t_kernel(tc, x_bytes, x_scale, mp, mq, mr, coef
         xgp = ctx.enter_context(tc.tile_pool(name="xgp", bufs=3))
         xcp = ctx.enter_context(tc.tile_pool(name="xcp", bufs=5))
         work = ctx.enter_context(tc.tile_pool(name="work", bufs=3))
-        zp = ctx.enter_context(tc.tile_pool(name="zp", bufs=2))
-        zcp = ctx.enter_context(tc.tile_pool(name="zcp", bufs=3))
+        zp = ctx.enter_context(tc.tile_pool(name="zp", bufs=3))
+        zcp = ctx.enter_context(tc.tile_pool(name="zcp", bufs=5))
         op = ctx.enter_context(tc.tile_pool(name="op", bufs=4))
         psum = ctx.enter_context(tc.psum_pool(name="psum", bufs=2))
         ctx.enter_context(tc.manual_schedule())
@@ -46,6 +46,15 @@ def tile_volterrathirdordermixer_t_kernel(tc, x_bytes, x_scale, mp, mq, mr, coef
         sc = const.tile([P, 4], F32, name="sc", align_bytes=64)
         load_x(0)
         nc.sync.dma_start(out=sc[:], in_=x_scale.rearrange("o (p t) z -> p (o t z)", t=4))
+        rows = const.tile([P, P], BF16, name="rows", align_bytes=64)
+        warm = const.tile([P, 1], F32, name="warm")
+        nc.vector.memset(rows[:], 0.0)
+        nc.vector.memset(warm[:], 0.0)
+        for v, vec in enumerate((coef[0], coef[1], gain)):
+            nc.sync.dma_start(
+                out=rows[4 * v : 4 * v + 4, :].rearrange("p (g i) -> p g i", i=8),
+                in_=vec.rearrange("(g j i) -> j g i", j=4, i=8),
+            )
         m_raw = []
         for i, m in enumerate((mr, mq, mp)):
             m_sb = const.tile([P, 2, S], BF16, name="m_sb%d" % i, align_bytes=64)
@@ -54,16 +63,7 @@ def tile_volterrathirdordermixer_t_kernel(tc, x_bytes, x_scale, mp, mq, mr, coef
         load_x(1)
         load_x(2)
 
-        rows = const.tile([P, P], BF16, name="rows", align_bytes=64)
-        warm = const.tile([P, 1], F32, name="warm")
-        nc.vector.memset(warm[:], 0.0)
-        nc.vector.memset(rows[:], 0.0)
         nc.scalar.activation(out=warm[:], in_=warm[:], func=IDENT)
-        for v, vec in enumerate((coef[0], coef[1], gain)):
-            nc.scalar.dma_start(
-                out=rows[4 * v : 4 * v + 4, :].rearrange("p (g i) -> p g i", i=8),
-                in_=vec.rearrange("(g j i) -> j g i", j=4, i=8),
-            )
         ident = const.tile([P, P], F32, name="ident", align_bytes=64)
         make_identity(nc, ident[:])
         ident_b = const.tile([P, P], BF16, name="ident_b", align_bytes=64)
@@ -95,8 +95,8 @@ def tile_volterrathirdordermixer_t_kernel(tc, x_bytes, x_scale, mp, mq, mr, coef
             x_il = xgp.tile([P, 4 * D], BF16, name="x_il", align_bytes=64)
             xg[b] = x_il
             nc.vector.tensor_copy(
-                out=x_il[:].rearrange("p (j g i t) -> p g j i t", j=4, g=16, i=8, t=4),
-                in_=xs[b][:].rearrange("p t (g j i) -> p g j i t", g=16, j=4, i=8),
+                out=x_il[:].rearrange("p (j g i t) -> p g j t i", j=4, g=16, i=8, t=4),
+                in_=xs[b][:].rearrange("p t (g j i) -> p g j t i", g=16, j=4, i=8),
             )
 
         def xq(b):
@@ -182,12 +182,24 @@ def tile_volterrathirdordermixer_t_kernel(tc, x_bytes, x_scale, mp, mq, mr, coef
 
         zil, zc, zsc = {}, {}, {}
 
-        def zint(gi, k):
-            z_il = zcp.tile([P, T, 4], BF16, name="z_il", align_bytes=64)
-            nc.vector.tensor_copy(
-                out=z_il[:], in_=zr[gi][:, :, k * T : (k + 1) * T].rearrange("p j t -> p t j")
+        def zint(gi, k, engine, halves=(0, 1)):
+            if halves[0] == 0:
+                z_il = zcp.tile([P, T, 4], BF16, name="z_il", align_bytes=64)
+                zil[gi, k] = z_il
+            t0, t1 = halves[0] * P, (halves[-1] + 1) * P
+            dst = zil[gi, k][:, t0:t1, :]
+            z_src = zr[gi][:, :, k * T + t0 : k * T + t1].rearrange("p j t -> p t j")
+            if engine == "V":
+                nc.vector.tensor_copy(out=dst, in_=z_src)
+            elif engine == "S":
+                nc.scalar.copy(out=dst, in_=z_src)
+            else:
+                nc.gpsimd.tensor_scalar(out=dst, in0=z_src, scalar1=1.0, scalar2=0.0, op0=MULT, op1=ADD)
+
+        def gate(b):
+            nc.gpsimd.tensor_scalar(
+                out=gate_sb[:], in0=xg[b][:, 4 * D - 1 : 4 * D], scalar1=1.0, scalar2=0.0, op0=MULT, op1=ADD
             )
-            zil[gi, k] = z_il
 
         def zq(gi, k):
             z_q = zcp.tile([P, T], U32, name="z_q", align_bytes=64)
@@ -218,112 +230,123 @@ def tile_volterrathirdordermixer_t_kernel(tc, x_bytes, x_scale, mp, mq, mr, coef
             nc.scalar.copy(out=o_sb[:], in_=O[gi, k][:])
             nc.sync.dma_start(out=out[GROUPS[gi][k]].rearrange("(p c) e -> p c e", c=2), in_=o_sb[:])
 
+        gate_sb = const.tile([P, 1], F32, name="gate_sb")
+        cf = const.tile([P, 12], F32, name="cf", align_bytes=64)
+        gc = const.tile([P, 8], F32, name="gc", align_bytes=64)
+        c_ps = psum.tile([P, P], BF16, name="c_ps", tag="O")
+        nc.vector.tensor_copy(out=ident_b[:], in_=ident[:])
+        widen(0, 1, "V")
         widen(0, 2, "V")
         widen(0, 3, "V")
         widen(0, 0, "S")
-        widen(0, 1, "S")
         m_turn(0)
         xint(0)
-        m_turn(1)
-        nc.vector.tensor_copy(out=ident_b[:], in_=ident[:])
-        c_ps = psum.tile([P, P], BF16, name="c_ps", tag="O")
         nc.tensor.transpose(c_ps[:], rows[:], ident_b[:])
-        cf = const.tile([P, 12], F32, name="cf", align_bytes=64)
+        m_turn(1)
         nc.vector.tensor_copy(out=cf[:], in_=c_ps[:, 0:12])
         m_quant(0)
         xq(0)
-        gc = const.tile([P, 8], F32, name="gc", align_bytes=64)
         nc.vector.tensor_tensor(out=gc[:, 0:4], in0=cf[:, 0:4], in1=cf[:, 8:12], op=MULT)
         nc.vector.tensor_tensor(out=gc[:, 4:8], in0=cf[:, 4:8], in1=cf[:, 8:12], op=MULT)
         m_turn(2)
         m_quant(1)
-        m_quant(2)
         widen(1, 2, "V")
+        m_quant(2)
         widen(1, 3, "V")
 
         units = [(gi, j) for gi in range(len(GROUPS)) for j in range(4)]
         last = len(GROUPS) - 1
         total = len(units)
-        mm(0)
-        h_of(0)
         w_il = const.tile([P, E, 4], BF16, name="w_il", align_bytes=64)
         w_q = const.tile([P, E], U32, name="w_q", align_bytes=64)
         w_s = const.tile([P, E], U8, name="w_s", align_bytes=64)
-        widen(1, 0, "S")
-        widen(1, 1, "S")
+
+        def w_int():
+            nc.vector.tensor_copy(out=w_il[:], in_=w_raw[:].rearrange("p j e -> p e j"))
+
+        def w_quant():
+            nc.vector.quantize_mx(
+                out=w_q[:].bitcast(X4), scales=w_s[:], in_=w_il[:].rearrange("p e j -> p (e j)")
+            )
+
+        def wid(b, *ts):
+            for t in ts:
+                widen(b, t, "S")
+
+        before = [[] for n in range(total + 12)]
+        after = [[] for n in range(total + 12)]
+
+        def put(where, n, *call):
+            where[n].append(call)
+
+        start = [4 * gi for gi in range(len(GROUPS))]
+        put(before, 2, w_int)
+        put(before, 6, w_quant)
+        for gi in range(1, last + 1):
+            bs, f = GROUPS[gi], start[gi]
+            if len(bs) == 1:
+                put(before, f - 4, xint, bs[0])
+                put(before, f - 3, xq, bs[0])
+                if gi > 1:
+                    put(after, f - 6, wid, bs[0], 0, 1)
+                    put(after, f - 5, wid, bs[0], 2, 3)
+            else:
+                put(before, f - 5, xint, bs[0])
+                put(before, f - 4, xq, bs[0])
+                put(before, f - 4, xint, bs[1])
+                put(before, f - 3, xq, bs[1])
+                if gi > 2:
+                    put(after, f - 8, wid, bs[0], 0, 1)
+                put(after, f - 7, wid, bs[0], 2, 3)
+                put(after, f - 6, wid, bs[1], 0, 1)
+                put(after, f - 5, wid, bs[1], 2, 3)
+        for gi in range(last):
+            f = start[gi]
+            if len(GROUPS[gi]) == 1:
+                put(after, f + 4, zint, gi, 0, "S")
+                put(before, f + 6, zq, gi, 0)
+                put(after, f + 6, omm, gi, 0)
+                put(after, f + 7, ocopy, gi, 0)
+            elif gi <= 4:
+                put(after, f + 4, zint, gi, 0, "S")
+                put(before, f + 6, zq, gi, 0)
+                put(after, f + 6, omm, gi, 0)
+                put(after, f + 7, ocopy, gi, 0)
+                put(before, f + 4, gate, GROUPS[gi + 2][1])
+                put(before, f + 4, zint, gi, 1, "G", (0,))
+                put(before, f + 7, gate, GROUPS[gi + 3][0])
+                put(before, f + 7, zint, gi, 1, "G", (1,))
+                put(before, f + 9, zq, gi, 1)
+                put(after, f + 9, omm, gi, 1)
+                put(after, f + 10, ocopy, gi, 1)
+            else:
+                put(after, f + 4, zint, gi, 0, "S")
+                put(after, f + 5, zint, gi, 1, "S")
+                put(before, f + 6, zq, gi, 0)
+                put(after, f + 6, omm, gi, 0)
+                put(after, f + 7, ocopy, gi, 0)
+                put(before, f + 7, zq, gi, 1)
+                put(after, f + 7, omm, gi, 1)
+                put(after, f + 8, ocopy, gi, 1)
+        mm(0)
+        h_of(0)
+        wid(1, 0, 1)
         mm(1)
         h_of(1)
+        wid(2, 0, 1)
         first(0)
         for n, (gi, j) in enumerate(units):
             if n + 1 < total:
                 first(n + 1)
             second(n)
-            nxt = GROUPS[gi + 1] if gi + 1 <= last else []
-            nn = GROUPS[gi + 2] if gi + 2 <= last else []
-            prev = GROUPS[gi - 1] if gi > 0 else []
-            if gi == 0:
-                if j == 0:
-                    xint(1)
-                elif j == 1:
-                    xq(1)
-                    xint(2)
-                elif j == 2:
-                    xq(2)
-                else:
-                    nc.vector.tensor_copy(out=w_il[:], in_=w_raw[:].rearrange("p j e -> p e j"))
-                    xint(3)
-            elif nxt:
-                if j == 0:
-                    xq(nxt[0])
-                    if len(nxt) > 1:
-                        xint(nxt[1])
-                elif j == 1:
-                    if len(nxt) > 1:
-                        xq(nxt[1])
-                    if gi == 1:
-                        nc.vector.quantize_mx(
-                            out=w_q[:].bitcast(X4), scales=w_s[:], in_=w_il[:].rearrange("p e j -> p (e j)")
-                        )
-                    zint(gi - 1, 0)
-                elif j == 2:
-                    if len(prev) > 1:
-                        zint(gi - 1, 1)
-                        zq(gi - 1, 0)
-                else:
-                    if nn:
-                        xint(nn[0])
-                    if len(prev) > 1:
-                        zq(gi - 1, 1)
-                    else:
-                        zq(gi - 1, 0)
-            else:
-                if j == 0:
-                    zint(gi - 1, 0)
-                elif j == 1:
-                    zint(gi - 1, 1)
-                    zq(gi - 1, 0)
-                elif j == 2:
-                    zq(gi - 1, 1)
+            for fn, *args in before[n]:
+                fn(*args)
             if n + 2 < total:
                 mm(n + 2)
                 h_of(n + 2)
-            if j == 0 and gi >= 2:
-                ocopy(gi - 2, len(GROUPS[gi - 2]) - 1)
-            if j == 2 and len(prev) > 1:
-                omm(gi - 1, 0)
-            if j == 3 and prev:
-                if len(prev) > 1:
-                    ocopy(gi - 1, 0)
-                omm(gi - 1, len(prev) - 1)
-            if gi == 0:
-                todo = [[(2, t) for t in range(4)], [(3, 0), (3, 1)], [(3, 2), (3, 3)], [(4, t) for t in range(4)]][j]
-            else:
-                ahead = [(b, t) for b in nn for t in range(4)]
-                todo = ahead[2 * j : 2 * j + 2]
-            for b, t in todo:
-                widen(b, t, "S")
-        zint(last, 0)
-        ocopy(last - 1, 1)
+            for fn, *args in after[n]:
+                fn(*args)
+        zint(last, 0, "V")
         zq(last, 0)
         omm(last, 0)
         ocopy(last, 0)

@@ -5,6 +5,7 @@ from concourse.masks import make_identity
 
 NB, S, D, T, E = 16, 512, 512, 256, 256
 P = 128
+AHEAD = 0
 FLOPS = NB * (2 * 3 * T * S * D + 2 * T * D * E)
 
 F32 = mybir.dt.float32
@@ -18,33 +19,34 @@ IDENT = mybir.ActivationFunctionType.Identity
 ADD = mybir.AluOpType.add
 MULT = mybir.AluOpType.mult
 
-GROUPS = [[0], [1]] + [[b, b + 1] for b in range(2, 14, 2)] + [[14], [15]]
+ZHOW = {}
 
 
 def tile_volterrathirdordermixer_t_kernel(tc, x_bytes, x_scale, mp, mq, mr, coef, gain, wo, out):
     nc = tc.nc
     with ExitStack() as ctx:
         const = ctx.enter_context(tc.tile_pool(name="const", bufs=1))
-        xbp = ctx.enter_context(tc.tile_pool(name="xbp", bufs=NB))
-        xsp = ctx.enter_context(tc.tile_pool(name="xsp", bufs=6))
+        xbp = ctx.enter_context(tc.tile_pool(name="xbp", bufs=NB // 2))
+        xsp = ctx.enter_context(tc.tile_pool(name="xsp", bufs=3))
         xgp = ctx.enter_context(tc.tile_pool(name="xgp", bufs=3))
         xcp = ctx.enter_context(tc.tile_pool(name="xcp", bufs=5))
         work = ctx.enter_context(tc.tile_pool(name="work", bufs=3))
         zp = ctx.enter_context(tc.tile_pool(name="zp", bufs=3))
-        zcp = ctx.enter_context(tc.tile_pool(name="zcp", bufs=5))
+        zcp = ctx.enter_context(tc.tile_pool(name="zcp", bufs=4))
         op = ctx.enter_context(tc.tile_pool(name="op", bufs=4))
         psum = ctx.enter_context(tc.psum_pool(name="psum", bufs=2))
         ctx.enter_context(tc.manual_schedule())
 
         xb = {}
 
-        def load_x(b):
-            x_codes = xbp.tile([P, 4 * D], U8, name="x_codes", align_bytes=64)
-            nc.sync.dma_start(out=x_codes[:], in_=x_bytes[b].rearrange("(p t) d -> p (t d)", t=4))
+        def load_x(b, w):
+            x_codes = xbp.tile([P, 4, w, D], U8, name="x_codes%d" % w, align_bytes=64)
+            for k in range(w):
+                nc.sync.dma_start(out=x_codes[:, :, k, :], in_=x_bytes[b + k].rearrange("(p t) d -> p t d", t=4))
             xb[b] = x_codes
 
         sc = const.tile([P, 4], F32, name="sc", align_bytes=64)
-        load_x(0)
+        load_x(0, 1)
         nc.sync.dma_start(out=sc[:], in_=x_scale.rearrange("o (p t) z -> p (o t z)", t=4))
         rows = const.tile([P, P], BF16, name="rows", align_bytes=64)
         warm = const.tile([P, 1], F32, name="warm")
@@ -60,8 +62,9 @@ def tile_volterrathirdordermixer_t_kernel(tc, x_bytes, x_scale, mp, mq, mr, coef
             m_sb = const.tile([P, 2, S], BF16, name="m_sb%d" % i, align_bytes=64)
             nc.sync.dma_start(out=m_sb[:], in_=m.rearrange("(p c) k -> p c k", c=2))
             m_raw.append(m_sb)
-        load_x(1)
-        load_x(2)
+        load_x(1, 1)
+        load_x(2, 1)
+        load_x(3, 1)
 
         nc.scalar.activation(out=warm[:], in_=warm[:], func=IDENT)
         ident = const.tile([P, P], F32, name="ident", align_bytes=64)
@@ -74,30 +77,36 @@ def tile_volterrathirdordermixer_t_kernel(tc, x_bytes, x_scale, mp, mq, mr, coef
                 out=w_raw[8 * g : 8 * g + 8, :, :],
                 in_=wo[32 * g : 32 * g + 32, :].rearrange("(j i) e -> i j e", i=8),
             )
-        for b in range(3, NB):
-            load_x(b)
+        for b in range(4, NB, 2):
+            load_x(b, 2)
 
-        xs, xg, xc, xsc = {}, {}, {}, {}
+        xw, xs, xg, xc, xsc = {}, {}, {}, {}, {}
 
         def widen(b, t, engine):
+            w = 1 if b < 4 else 2
             if b not in xs:
-                x_wide = xsp.tile([P, 4, D], BF16, name="x_wide", align_bytes=64)
-                xs[b] = x_wide
-            src = xb[b][:, t * D : (t + 1) * D].bitcast(FP8)
+                x_wide = xsp.tile([P, 4, w, D], BF16, name="x_wide%d" % w, align_bytes=64)
+                for k in range(w):
+                    xs[b + k] = x_wide[:, :, k, :]
+                xw[b] = x_wide
+            dst = xw[b][:, t, :, :].rearrange("p b d -> p (b d)")
+            src = xb[b][:, t, :, :].rearrange("p b d -> p (b d)").bitcast(FP8)
             if engine == "S":
-                nc.scalar.activation(out=xs[b][:, t, :], in_=src, func=COPY, scale=sc[:, t : t + 1])
+                nc.scalar.activation(out=dst, in_=src, func=COPY, scale=sc[:, t : t + 1])
             else:
-                nc.vector.tensor_scalar(
-                    out=xs[b][:, t, :], in0=src, scalar1=sc[:, t : t + 1], scalar2=None, op0=MULT
-                )
+                nc.vector.tensor_scalar(out=dst, in0=src, scalar1=sc[:, t : t + 1], scalar2=None, op0=MULT)
+
+        def xhalf(b, j0, j1):
+            if j0 == 0:
+                x_il = xgp.tile([P, 4 * D], BF16, name="x_il", align_bytes=64)
+                xg[b] = x_il
+            nc.vector.tensor_copy(
+                out=xg[b][:].rearrange("p (j g i t) -> p g j t i", j=4, g=16, i=8, t=4)[:, :, j0:j1, :, :],
+                in_=xs[b].rearrange("p t (g j i) -> p g j t i", g=16, j=4, i=8)[:, :, j0:j1, :, :],
+            )
 
         def xint(b):
-            x_il = xgp.tile([P, 4 * D], BF16, name="x_il", align_bytes=64)
-            xg[b] = x_il
-            nc.vector.tensor_copy(
-                out=x_il[:].rearrange("p (j g i t) -> p g j t i", j=4, g=16, i=8, t=4),
-                in_=xs[b][:].rearrange("p t (g j i) -> p g j t i", g=16, j=4, i=8),
-            )
+            xhalf(b, 0, 4)
 
         def xq(b):
             x_q = xcp.tile([P, D], U32, name="x_q", align_bytes=64)
@@ -129,22 +138,20 @@ def tile_volterrathirdordermixer_t_kernel(tc, x_bytes, x_scale, mp, mq, mr, coef
             mc.append(m_q)
             msc.append(m_s)
 
-        R, Q, PP, H = {}, {}, {}, {}
-        zr = {}
+        R, Q, PP, H, U, zr = {}, {}, {}, {}, {}, {}
 
         def mm(n):
-            gi, j = units[n]
-            bs = GROUPS[gi]
-            w = len(bs) * T
-            r_ps = psum.tile([P, w], F32, name="r_ps", tag="R")
-            q_ps = psum.tile([P, w], F32, name="q_ps", tag="Q")
-            p_ps = psum.tile([P, w], F32, name="p_ps", tag="P")
+            b, j0 = n // 2, 2 * (n % 2)
+            r_ps = psum.tile([P, 2, T], F32, name="r_ps", tag="R")
+            q_ps = psum.tile([P, 2, T], F32, name="q_ps", tag="Q")
+            p_ps = psum.tile([P, 2, T], F32, name="p_ps", tag="P")
             for i, ps in enumerate((r_ps, q_ps, p_ps)):
-                for k, b in enumerate(bs):
+                for k in range(2):
+                    cols = slice((j0 + k) * P, (j0 + k + 1) * P)
                     nc.tensor.matmul_mx(
-                        out=ps[:, k * T : (k + 1) * T],
-                        lhsT=xc[b][:, j * P : (j + 1) * P].bitcast(X4),
-                        lhsT_scale=xsc[b][:, j * P : (j + 1) * P],
+                        out=ps[:, k, :],
+                        lhsT=xc[b][:, cols].bitcast(X4),
+                        lhsT_scale=xsc[b][:, cols],
                         rhs=mc[i][:].bitcast(X4),
                         rhs_scale=msc[i][:],
                         start=True,
@@ -153,84 +160,83 @@ def tile_volterrathirdordermixer_t_kernel(tc, x_bytes, x_scale, mp, mq, mr, coef
             R[n], Q[n], PP[n] = r_ps, q_ps, p_ps
 
         def h_of(n):
-            gi, j = units[n]
-            w = len(GROUPS[gi]) * T
-            h_sb = work.tile([P, w], F32, name="h_sb", align_bytes=64)
-            nc.scalar.activation(
-                out=h_sb[:], in_=R[n][:], func=IDENT, bias=gc[:, j : j + 1], scale=gc[:, 4 + j : 5 + j]
-            )
+            h_sb = work.tile([P, 2, T], F32, name="h_sb", align_bytes=64)
+            for k in range(2):
+                j = 2 * (n % 2) + k
+                nc.scalar.activation(
+                    out=h_sb[:, k, :], in_=R[n][:, k, :], func=IDENT, bias=gc[:, j : j + 1], scale=gc[:, 4 + j : 5 + j]
+                )
             H[n] = h_sb
 
-        U = {}
-
         def first(n):
-            gi, j = units[n]
-            w = len(GROUPS[gi]) * T
-            u_sb = work.tile([P, w], F32, name="u_sb", align_bytes=64)
+            u_sb = work.tile([P, 2, T], F32, name="u_sb", align_bytes=64)
             nc.vector.tensor_tensor(out=u_sb[:], in0=H[n][:], in1=Q[n][:], op=MULT)
             U[n] = u_sb
 
         def second(n):
-            gi, j = units[n]
-            w = len(GROUPS[gi]) * T
-            if j == 0:
-                z_raw = zp.tile([P, 4, w], BF16, name="z_raw", align_bytes=64)
-                zr[gi] = z_raw
-            nc.vector.scalar_tensor_tensor(
-                out=zr[gi][:, j, :], in0=U[n][:], scalar=cf[:, 8 + j : 9 + j], in1=PP[n][:], op0=ADD, op1=MULT
-            )
+            b = n // 2
+            if n % 2 == 0:
+                z_raw = zp.tile([P, 4, T], BF16, name="z_raw", align_bytes=64)
+                zr[b] = z_raw
+            for k in range(2):
+                j = 2 * (n % 2) + k
+                nc.vector.scalar_tensor_tensor(
+                    out=zr[b][:, j, :], in0=U[n][:, k, :], scalar=cf[:, 8 + j : 9 + j], in1=PP[n][:, k, :],
+                    op0=ADD, op1=MULT,
+                )
 
-        zil, zc, zsc = {}, {}, {}
+        zil, zc, zsc, ZT, O = {}, {}, {}, {}, {}
 
-        def zint(gi, k, engine, halves=(0, 1)):
-            if halves[0] == 0:
-                z_il = zcp.tile([P, T, 4], BF16, name="z_il", align_bytes=64)
-                zil[gi, k] = z_il
-            t0, t1 = halves[0] * P, (halves[-1] + 1) * P
-            dst = zil[gi, k][:, t0:t1, :]
-            z_src = zr[gi][:, :, k * T + t0 : k * T + t1].rearrange("p j t -> p t j")
+        def zint(b, engine):
+            z_il = zcp.tile([P, T, 4], BF16, name="z_il", align_bytes=64)
+            zil[b] = z_il
+            z_src = zr[b][:].rearrange("p j t -> p t j")
             if engine == "V":
-                nc.vector.tensor_copy(out=dst, in_=z_src)
-            elif engine == "S":
-                nc.scalar.copy(out=dst, in_=z_src)
+                nc.vector.tensor_copy(out=z_il[:], in_=z_src)
             else:
-                nc.gpsimd.tensor_scalar(out=dst, in0=z_src, scalar1=1.0, scalar2=0.0, op0=MULT, op1=ADD)
+                nc.scalar.copy(out=z_il[:], in_=z_src)
 
-        def gate(b):
-            nc.gpsimd.tensor_scalar(
-                out=gate_sb[:], in0=xg[b][:, 4 * D - 1 : 4 * D], scalar1=1.0, scalar2=0.0, op0=MULT, op1=ADD
-            )
+        def zturn(b):
+            zt_ps = psum.tile([P, T, 4], BF16, name="zt_ps", tag="O")
+            for c in range(2):
+                t = slice(c * P, (c + 1) * P)
+                nc.tensor.matmul(
+                    zt_ps[:, t, :].rearrange("p t j -> p j t"), lhsT=ident_b[:], rhs=zr[b][:, :, t], start=True, stop=True
+                )
+            ZT[b] = zt_ps
 
-        def zq(gi, k):
+        def zcopy(b):
+            z_il = zcp.tile([P, T, 4], BF16, name="z_il", align_bytes=64)
+            nc.scalar.copy(out=z_il[:].rearrange("p t j -> p (t j)"), in_=ZT[b][:].rearrange("p t j -> p (t j)"))
+            zil[b] = z_il
+
+        def zq(b):
             z_q = zcp.tile([P, T], U32, name="z_q", align_bytes=64)
             z_s = zcp.tile([P, T], U8, name="z_s", align_bytes=64)
             nc.vector.quantize_mx(
-                out=z_q[:].bitcast(X4), scales=z_s[:], in_=zil[gi, k][:].rearrange("p t j -> p (t j)")
+                out=z_q[:].bitcast(X4), scales=z_s[:], in_=zil[b][:].rearrange("p t j -> p (t j)")
             )
-            zc[gi, k], zsc[gi, k] = z_q, z_s
+            zc[b], zsc[b] = z_q, z_s
 
-        O = {}
-
-        def omm(gi, k):
+        def omm(b):
             o_ps = psum.tile([P, 2, E], F32, name="o_ps", tag="O")
             for c in range(2):
                 nc.tensor.matmul_mx(
                     out=o_ps[:, c, :],
-                    lhsT=zc[gi, k][:, c * P : (c + 1) * P].bitcast(X4),
-                    lhsT_scale=zsc[gi, k][:, c * P : (c + 1) * P],
+                    lhsT=zc[b][:, c * P : (c + 1) * P].bitcast(X4),
+                    lhsT_scale=zsc[b][:, c * P : (c + 1) * P],
                     rhs=w_q[:].bitcast(X4),
                     rhs_scale=w_s[:],
                     start=True,
                     stop=True,
                 )
-            O[gi, k] = o_ps
+            O[b] = o_ps
 
-        def ocopy(gi, k):
+        def ocopy(b):
             o_sb = op.tile([P, 2, E], F32, name="o_sb", align_bytes=64)
-            nc.scalar.copy(out=o_sb[:], in_=O[gi, k][:])
-            nc.sync.dma_start(out=out[GROUPS[gi][k]].rearrange("(p c) e -> p c e", c=2), in_=o_sb[:])
+            nc.scalar.copy(out=o_sb[:], in_=O[b][:])
+            nc.sync.dma_start(out=out[b].rearrange("(p c) e -> p c e", c=2), in_=o_sb[:])
 
-        gate_sb = const.tile([P, 1], F32, name="gate_sb")
         cf = const.tile([P, 12], F32, name="cf", align_bytes=64)
         gc = const.tile([P, 8], F32, name="gc", align_bytes=64)
         c_ps = psum.tile([P, P], BF16, name="c_ps", tag="O")
@@ -250,13 +256,13 @@ def tile_volterrathirdordermixer_t_kernel(tc, x_bytes, x_scale, mp, mq, mr, coef
         nc.vector.tensor_tensor(out=gc[:, 4:8], in0=cf[:, 4:8], in1=cf[:, 8:12], op=MULT)
         m_turn(2)
         m_quant(1)
-        widen(1, 2, "V")
+        widen(1, 0, "V")
+        widen(1, 1, "V")
         m_quant(2)
+        widen(1, 2, "V")
         widen(1, 3, "V")
 
-        units = [(gi, j) for gi in range(len(GROUPS)) for j in range(4)]
-        last = len(GROUPS) - 1
-        total = len(units)
+        total = 2 * NB
         w_il = const.tile([P, E, 4], BF16, name="w_il", align_bytes=64)
         w_q = const.tile([P, E], U32, name="w_q", align_bytes=64)
         w_s = const.tile([P, E], U8, name="w_s", align_bytes=64)
@@ -274,68 +280,45 @@ def tile_volterrathirdordermixer_t_kernel(tc, x_bytes, x_scale, mp, mq, mr, coef
                 widen(b, t, "S")
 
         before = [[] for n in range(total + 12)]
+        leading = [[] for n in range(total + 12)]
         after = [[] for n in range(total + 12)]
 
         def put(where, n, *call):
             where[n].append(call)
 
-        start = [4 * gi for gi in range(len(GROUPS))]
-        put(before, 2, w_int)
-        put(before, 6, w_quant)
-        for gi in range(1, last + 1):
-            bs, f = GROUPS[gi], start[gi]
-            if len(bs) == 1:
-                put(before, f - 4, xint, bs[0])
-                put(before, f - 3, xq, bs[0])
-                if gi > 1:
-                    put(after, f - 6, wid, bs[0], 0, 1)
-                    put(after, f - 5, wid, bs[0], 2, 3)
+        put(before, 0, w_int)
+        put(before, 2, w_quant)
+        for b in range(2, NB):
+            if b > 2:
+                put(before, 2 * b - 5, xint, b)
+            put(before, 2 * b - 3, xq, b)
+        for b in range(4, NB, 2):
+            for t in range(4):
+                put(after, max(0, 2 * b - 9 + t - AHEAD), wid, b, t)
+        for b in range(NB - 1):
+            how = ZHOW.get(b, "P")
+            if how == "P":
+                put(after, 2 * b + 1, zturn, b)
+                put(leading, 2 * b + 2, zcopy, b)
+            elif how == "S":
+                put(leading, 2 * b + 2, zint, b, "S")
             else:
-                put(before, f - 5, xint, bs[0])
-                put(before, f - 4, xq, bs[0])
-                put(before, f - 4, xint, bs[1])
-                put(before, f - 3, xq, bs[1])
-                if gi > 2:
-                    put(after, f - 8, wid, bs[0], 0, 1)
-                put(after, f - 7, wid, bs[0], 2, 3)
-                put(after, f - 6, wid, bs[1], 0, 1)
-                put(after, f - 5, wid, bs[1], 2, 3)
-        for gi in range(last):
-            f = start[gi]
-            if len(GROUPS[gi]) == 1:
-                put(after, f + 4, zint, gi, 0, "S")
-                put(before, f + 6, zq, gi, 0)
-                put(after, f + 6, omm, gi, 0)
-                put(after, f + 7, ocopy, gi, 0)
-            elif gi <= 4:
-                put(after, f + 4, zint, gi, 0, "S")
-                put(before, f + 6, zq, gi, 0)
-                put(after, f + 6, omm, gi, 0)
-                put(after, f + 7, ocopy, gi, 0)
-                put(before, f + 4, gate, GROUPS[gi + 2][1])
-                put(before, f + 4, zint, gi, 1, "G", (0,))
-                put(before, f + 7, gate, GROUPS[gi + 3][0])
-                put(before, f + 7, zint, gi, 1, "G", (1,))
-                put(before, f + 9, zq, gi, 1)
-                put(after, f + 9, omm, gi, 1)
-                put(after, f + 10, ocopy, gi, 1)
-            else:
-                put(after, f + 4, zint, gi, 0, "S")
-                put(after, f + 5, zint, gi, 1, "S")
-                put(before, f + 6, zq, gi, 0)
-                put(after, f + 6, omm, gi, 0)
-                put(after, f + 7, ocopy, gi, 0)
-                put(before, f + 7, zq, gi, 1)
-                put(after, f + 7, omm, gi, 1)
-                put(after, f + 8, ocopy, gi, 1)
+                put(before, 2 * b + 3, zint, b, "V")
+            put(before, 2 * b + 4, zq, b)
+            put(after, 2 * b + 4, omm, b)
+            put(leading, 2 * b + 5, ocopy, b)
         mm(0)
         h_of(0)
-        wid(1, 0, 1)
+        wid(2, 0, 1, 2)
+        xint(1)
         mm(1)
         h_of(1)
-        wid(2, 0, 1)
+        wid(2, 3)
+        wid(3, 0, 1, 2, 3)
         first(0)
-        for n, (gi, j) in enumerate(units):
+        xq(1)
+        xint(2)
+        for n in range(total):
             if n + 1 < total:
                 first(n + 1)
             second(n)
@@ -344,9 +327,30 @@ def tile_volterrathirdordermixer_t_kernel(tc, x_bytes, x_scale, mp, mq, mr, coef
             if n + 2 < total:
                 mm(n + 2)
                 h_of(n + 2)
-            for fn, *args in after[n]:
+            for fn, *args in leading[n] + after[n]:
                 fn(*args)
-        zint(last, 0, "V")
-        zq(last, 0)
-        omm(last, 0)
-        ocopy(last, 0)
+        for n in range(total, total + 12):
+            for fn, *args in before[n] + leading[n] + after[n]:
+                fn(*args)
+        b = NB - 1
+        zl = []
+        for c in range(2):
+            z_il = zcp.tile([P, P, 4], BF16, name="z_il%d" % c, align_bytes=64)
+            z_src = zr[b][:, :, c * P : (c + 1) * P].rearrange("p j t -> p t j")
+            nc.vector.tensor_copy(out=z_il[:], in_=z_src)
+            zl.append(z_il)
+        for c in range(2):
+            z_q = zcp.tile([P, P], U32, name="z_q%d" % c, align_bytes=64)
+            z_s = zcp.tile([P, P], U8, name="z_s%d" % c, align_bytes=64)
+            nc.vector.quantize_mx(out=z_q[:].bitcast(X4), scales=z_s[:], in_=zl[c][:].rearrange("p t j -> p (t j)"))
+            o_ps = psum.tile([P, E], F32, name="o_ps", tag="O")
+            nc.tensor.matmul_mx(
+                out=o_ps[:], lhsT=z_q[:].bitcast(X4), lhsT_scale=z_s[:], rhs=w_q[:].bitcast(X4), rhs_scale=w_s[:],
+                start=True, stop=True,
+            )
+            o_sb = op.tile([P, E], F32, name="o_sb%d" % c, align_bytes=64)
+            if c == 0:
+                nc.scalar.copy(out=o_sb[:], in_=o_ps[:])
+            else:
+                nc.vector.tensor_copy(out=o_sb[:], in_=o_ps[:])
+            nc.sync.dma_start(out=out[b].rearrange("(p c) e -> p c e", c=2)[:, c, :], in_=o_sb[:])

@@ -5,7 +5,6 @@ from concourse.masks import make_identity
 
 NB, S, D, T, E = 16, 512, 512, 256, 256
 P = 128
-AHEAD = 0
 FLOPS = NB * (2 * 3 * T * S * D + 2 * T * D * E)
 
 F32 = mybir.dt.float32
@@ -15,132 +14,131 @@ U8 = mybir.dt.uint8
 FP8 = mybir.dt.float8_e4m3fn
 X4 = mybir.dt.float8_e4m3fn_x4
 COPY = mybir.ActivationFunctionType.Copy
-IDENT = mybir.ActivationFunctionType.Identity
+IDENTITY = mybir.ActivationFunctionType.Identity
 ADD = mybir.AluOpType.add
 MULT = mybir.AluOpType.mult
 
-ZHOW = {}
+STEPS = 2 * NB
+SINGLE = 4
+LAST = NB - 1
+DIRECT = NB - 3
 
 
 def tile_volterrathirdordermixer_t_kernel(tc, x_bytes, x_scale, mp, mq, mr, coef, gain, wo, out):
     nc = tc.nc
     with ExitStack() as ctx:
         const = ctx.enter_context(tc.tile_pool(name="const", bufs=1))
-        xbp = ctx.enter_context(tc.tile_pool(name="xbp", bufs=NB // 2))
-        xsp = ctx.enter_context(tc.tile_pool(name="xsp", bufs=3))
-        xgp = ctx.enter_context(tc.tile_pool(name="xgp", bufs=3))
-        xcp = ctx.enter_context(tc.tile_pool(name="xcp", bufs=5))
-        work = ctx.enter_context(tc.tile_pool(name="work", bufs=3))
-        zp = ctx.enter_context(tc.tile_pool(name="zp", bufs=3))
-        zcp = ctx.enter_context(tc.tile_pool(name="zcp", bufs=4))
-        op = ctx.enter_context(tc.tile_pool(name="op", bufs=4))
+        bytes_pool = ctx.enter_context(tc.tile_pool(name="bytes_pool", bufs=8))
+        wide_pool = ctx.enter_context(tc.tile_pool(name="wide_pool", bufs=3))
+        x_pool = ctx.enter_context(tc.tile_pool(name="x_pool", bufs=3))
+        xq_pool = ctx.enter_context(tc.tile_pool(name="xq_pool", bufs=5))
+        poly = ctx.enter_context(tc.tile_pool(name="poly", bufs=3))
+        z_pool = ctx.enter_context(tc.tile_pool(name="z_pool", bufs=3))
+        zq_pool = ctx.enter_context(tc.tile_pool(name="zq_pool", bufs=4))
+        out_pool = ctx.enter_context(tc.tile_pool(name="out_pool", bufs=4))
         psum = ctx.enter_context(tc.psum_pool(name="psum", bufs=2))
         ctx.enter_context(tc.manual_schedule())
 
-        xb = {}
+        x_raw = {}
 
-        def load_x(b, w):
-            x_codes = xbp.tile([P, 4, w, D], U8, name="x_codes%d" % w, align_bytes=64)
-            for k in range(w):
-                nc.sync.dma_start(out=x_codes[:, :, k, :], in_=x_bytes[b + k].rearrange("(p t) d -> p t d", t=4))
-            xb[b] = x_codes
+        def load_x(b, width):
+            codes = bytes_pool.tile([P, 4, width, D], U8, name="codes%d" % width, align_bytes=64)
+            for k in range(width):
+                nc.sync.dma_start(out=codes[:, :, k, :], in_=x_bytes[b + k].rearrange("(p t) d -> p t d", t=4))
+            x_raw[b] = codes
 
-        sc = const.tile([P, 4], F32, name="sc", align_bytes=64)
         load_x(0, 1)
-        nc.sync.dma_start(out=sc[:], in_=x_scale.rearrange("o (p t) z -> p (o t z)", t=4))
-        rows = const.tile([P, P], BF16, name="rows", align_bytes=64)
-        warm = const.tile([P, 1], F32, name="warm")
-        nc.vector.memset(rows[:], 0.0)
-        nc.vector.memset(warm[:], 0.0)
+        scale = const.tile([P, 4], F32, name="scale", align_bytes=64)
+        nc.sync.dma_start(out=scale[:], in_=x_scale.rearrange("o (p t) z -> p (o t z)", t=4))
+
+        vec_rows = const.tile([P, P], BF16, name="vec_rows", align_bytes=64)
+        first_act = const.tile([P, 1], F32, name="first_act")
+        nc.vector.memset(vec_rows[:], 0.0)
+        nc.vector.memset(first_act[:], 0.0)
         for v, vec in enumerate((coef[0], coef[1], gain)):
             nc.sync.dma_start(
-                out=rows[4 * v : 4 * v + 4, :].rearrange("p (g i) -> p g i", i=8),
+                out=vec_rows[4 * v : 4 * v + 4, :].rearrange("p (g i) -> p g i", i=8),
                 in_=vec.rearrange("(g j i) -> j g i", j=4, i=8),
             )
         m_raw = []
         for i, m in enumerate((mr, mq, mp)):
-            m_sb = const.tile([P, 2, S], BF16, name="m_sb%d" % i, align_bytes=64)
-            nc.sync.dma_start(out=m_sb[:], in_=m.rearrange("(p c) k -> p c k", c=2))
-            m_raw.append(m_sb)
-        load_x(1, 1)
-        load_x(2, 1)
-        load_x(3, 1)
+            m_rows = const.tile([P, 2, S], BF16, name="m_rows%d" % i, align_bytes=64)
+            nc.sync.dma_start(out=m_rows[:], in_=m.rearrange("(p c) k -> p c k", c=2))
+            m_raw.append(m_rows)
+        for b in range(1, SINGLE):
+            load_x(b, 1)
 
-        nc.scalar.activation(out=warm[:], in_=warm[:], func=IDENT)
-        ident = const.tile([P, P], F32, name="ident", align_bytes=64)
-        make_identity(nc, ident[:])
-        ident_b = const.tile([P, P], BF16, name="ident_b", align_bytes=64)
+        nc.scalar.activation(out=first_act[:], in_=first_act[:], func=IDENTITY)
+        ident_f32 = const.tile([P, P], F32, name="ident_f32", align_bytes=64)
+        make_identity(nc, ident_f32[:])
+        ident_bf16 = const.tile([P, P], BF16, name="ident_bf16", align_bytes=64)
 
-        w_raw = const.tile([P, 4, E], BF16, name="w_raw", align_bytes=64)
+        wo_rows = const.tile([P, 4, E], BF16, name="wo_rows", align_bytes=64)
         for g in range(16):
             nc.sync.dma_start(
-                out=w_raw[8 * g : 8 * g + 8, :, :],
+                out=wo_rows[8 * g : 8 * g + 8, :, :],
                 in_=wo[32 * g : 32 * g + 32, :].rearrange("(j i) e -> i j e", i=8),
             )
-        for b in range(4, NB, 2):
+        for b in range(SINGLE, NB, 2):
             load_x(b, 2)
 
-        xw, xs, xg, xc, xsc = {}, {}, {}, {}, {}
+        x_wide, x_rows, x_words, x_codes, x_scales = {}, {}, {}, {}, {}
 
-        def widen(b, t, engine):
-            w = 1 if b < 4 else 2
-            if b not in xs:
-                x_wide = xsp.tile([P, 4, w, D], BF16, name="x_wide%d" % w, align_bytes=64)
-                for k in range(w):
-                    xs[b + k] = x_wide[:, :, k, :]
-                xw[b] = x_wide
-            dst = xw[b][:, t, :, :].rearrange("p b d -> p (b d)")
-            src = xb[b][:, t, :, :].rearrange("p b d -> p (b d)").bitcast(FP8)
-            if engine == "S":
-                nc.scalar.activation(out=dst, in_=src, func=COPY, scale=sc[:, t : t + 1])
+        def widen(engine, b, t):
+            width = 1 if b < SINGLE else 2
+            if b not in x_wide:
+                wide = wide_pool.tile([P, 4, width, D], BF16, name="wide%d" % width, align_bytes=64)
+                x_wide[b] = wide
+                for k in range(width):
+                    x_rows[b + k] = wide[:, :, k, :]
+            dst = x_wide[b][:, t, :, :].rearrange("p b d -> p (b d)")
+            src = x_raw[b][:, t, :, :].rearrange("p b d -> p (b d)").bitcast(FP8)
+            if engine == "scalar":
+                nc.scalar.activation(out=dst, in_=src, func=COPY, scale=scale[:, t : t + 1])
             else:
-                nc.vector.tensor_scalar(out=dst, in0=src, scalar1=sc[:, t : t + 1], scalar2=None, op0=MULT)
+                nc.vector.tensor_scalar(out=dst, in0=src, scalar1=scale[:, t : t + 1], scalar2=None, op0=MULT)
 
-        def xhalf(b, j0, j1):
-            if j0 == 0:
-                x_il = xgp.tile([P, 4 * D], BF16, name="x_il", align_bytes=64)
-                xg[b] = x_il
+        def interleave_x(b):
+            words = x_pool.tile([P, 4 * D], BF16, name="words", align_bytes=64)
             nc.vector.tensor_copy(
-                out=xg[b][:].rearrange("p (j g i t) -> p g j t i", j=4, g=16, i=8, t=4)[:, :, j0:j1, :, :],
-                in_=xs[b].rearrange("p t (g j i) -> p g j t i", g=16, j=4, i=8)[:, :, j0:j1, :, :],
+                out=words[:].rearrange("p (j g i t) -> p g j t i", j=4, g=16, i=8, t=4),
+                in_=x_rows[b].rearrange("p t (g j i) -> p g j t i", g=16, j=4, i=8),
             )
+            x_words[b] = words
 
-        def xint(b):
-            xhalf(b, 0, 4)
+        def quantize_x(b):
+            codes = xq_pool.tile([P, D], U32, name="x_q", align_bytes=64)
+            scales = xq_pool.tile([P, D], U8, name="x_qs", align_bytes=64)
+            nc.vector.quantize_mx(out=codes[:].bitcast(X4), scales=scales[:], in_=x_words[b][:])
+            x_codes[b], x_scales[b] = codes, scales
 
-        def xq(b):
-            x_q = xcp.tile([P, D], U32, name="x_q", align_bytes=64)
-            x_qs = xcp.tile([P, D], U8, name="x_qs", align_bytes=64)
-            nc.vector.quantize_mx(out=x_q[:].bitcast(X4), scales=x_qs[:], in_=xg[b][:])
-            xc[b], xsc[b] = x_q, x_qs
+        m_words, m_codes, m_scales = [], [], []
 
-        mc, msc = [], []
-        m_il = []
-
-        def m_turn(i):
-            m_ps = psum.tile([P, 2, 2, P], F32, name="m_ps", tag="RQP"[i])
-            words = m_raw[i]
+        def turn_m(i):
+            turned = psum.tile([P, 2, 2, P], F32, name="turned", tag="RQP"[i])
             for c in range(2):
-                wv = words[:, c, :].bitcast(F32)
+                words = m_raw[i][:, c, :].bitcast(F32)
                 for u in range(2):
-                    nc.tensor.transpose(m_ps[:, c, u, :], wv[:, u : S // 2 : 2], ident[:])
-            m_g = const.tile([P, T, 4], BF16, name="m_g%d" % i, align_bytes=64)
-            dst = m_g[:].rearrange("p n t -> p (n t)").bitcast(F32).rearrange("p (c r u) -> p c r u", c=2, u=2)
-            nc.scalar.copy(out=dst, in_=m_ps[:].rearrange("p c u r -> p c r u"))
-            m_il.append(m_g)
-
-        def m_quant(i):
-            m_q = const.tile([P, T], U32, name="m_q%d" % i, align_bytes=64)
-            m_s = const.tile([P, T], U8, name="m_s%d" % i, align_bytes=64)
-            nc.vector.quantize_mx(
-                out=m_q[:].bitcast(X4), scales=m_s[:], in_=m_il[i][:].rearrange("p n t -> p (n t)")
+                    nc.tensor.transpose(turned[:, c, u, :], words[:, u : S // 2 : 2], ident_f32[:])
+            grouped = const.tile([P, T, 4], BF16, name="m_words%d" % i, align_bytes=64)
+            dst = grouped[:].rearrange("p n t -> p (n t)").bitcast(F32)
+            nc.scalar.copy(
+                out=dst.rearrange("p (c n u) -> p c n u", c=2, u=2), in_=turned[:].rearrange("p c u n -> p c n u")
             )
-            mc.append(m_q)
-            msc.append(m_s)
+            m_words.append(grouped)
 
-        R, Q, PP, H, U, zr = {}, {}, {}, {}, {}, {}
+        def quantize_m(i):
+            codes = const.tile([P, T], U32, name="m_q%d" % i, align_bytes=64)
+            scales = const.tile([P, T], U8, name="m_qs%d" % i, align_bytes=64)
+            nc.vector.quantize_mx(
+                out=codes[:].bitcast(X4), scales=scales[:], in_=m_words[i][:].rearrange("p n t -> p (n t)")
+            )
+            m_codes.append(codes)
+            m_scales.append(scales)
 
-        def mm(n):
+        r_sum, q_sum, p_sum, h_val, u_val, z_tile = {}, {}, {}, {}, {}, {}
+
+        def products(n):
             b, j0 = n // 2, 2 * (n % 2)
             r_ps = psum.tile([P, 2, T], F32, name="r_ps", tag="R")
             q_ps = psum.tile([P, 2, T], F32, name="q_ps", tag="Q")
@@ -150,207 +148,212 @@ def tile_volterrathirdordermixer_t_kernel(tc, x_bytes, x_scale, mp, mq, mr, coef
                     cols = slice((j0 + k) * P, (j0 + k + 1) * P)
                     nc.tensor.matmul_mx(
                         out=ps[:, k, :],
-                        lhsT=xc[b][:, cols].bitcast(X4),
-                        lhsT_scale=xsc[b][:, cols],
-                        rhs=mc[i][:].bitcast(X4),
-                        rhs_scale=msc[i][:],
+                        lhsT=x_codes[b][:, cols].bitcast(X4),
+                        lhsT_scale=x_scales[b][:, cols],
+                        rhs=m_codes[i][:].bitcast(X4),
+                        rhs_scale=m_scales[i][:],
                         start=True,
                         stop=True,
                     )
-            R[n], Q[n], PP[n] = r_ps, q_ps, p_ps
+            r_sum[n], q_sum[n], p_sum[n] = r_ps, q_ps, p_ps
 
-        def h_of(n):
-            h_sb = work.tile([P, 2, T], F32, name="h_sb", align_bytes=64)
+        def third_order(n):
+            h = poly.tile([P, 2, T], F32, name="h", align_bytes=64)
             for k in range(2):
                 j = 2 * (n % 2) + k
                 nc.scalar.activation(
-                    out=h_sb[:, k, :], in_=R[n][:, k, :], func=IDENT, bias=gc[:, j : j + 1], scale=gc[:, 4 + j : 5 + j]
+                    out=h[:, k, :],
+                    in_=r_sum[n][:, k, :],
+                    func=IDENTITY,
+                    bias=gain_coef[:, j : j + 1],
+                    scale=gain_coef[:, 4 + j : 5 + j],
                 )
-            H[n] = h_sb
+            h_val[n] = h
 
-        def first(n):
-            u_sb = work.tile([P, 2, T], F32, name="u_sb", align_bytes=64)
-            nc.vector.tensor_tensor(out=u_sb[:], in0=H[n][:], in1=Q[n][:], op=MULT)
-            U[n] = u_sb
+        def times_q(n):
+            u = poly.tile([P, 2, T], F32, name="u", align_bytes=64)
+            nc.vector.tensor_tensor(out=u[:], in0=h_val[n][:], in1=q_sum[n][:], op=MULT)
+            u_val[n] = u
 
-        def second(n):
+        def times_p(n):
             b = n // 2
             if n % 2 == 0:
-                z_raw = zp.tile([P, 4, T], BF16, name="z_raw", align_bytes=64)
-                zr[b] = z_raw
+                z_rows = z_pool.tile([P, 4, T], BF16, name="z_rows", align_bytes=64)
+                z_tile[b] = z_rows
             for k in range(2):
                 j = 2 * (n % 2) + k
                 nc.vector.scalar_tensor_tensor(
-                    out=zr[b][:, j, :], in0=U[n][:, k, :], scalar=cf[:, 8 + j : 9 + j], in1=PP[n][:, k, :],
-                    op0=ADD, op1=MULT,
+                    out=z_tile[b][:, j, :],
+                    in0=u_val[n][:, k, :],
+                    scalar=vec_cols[:, 8 + j : 9 + j],
+                    in1=p_sum[n][:, k, :],
+                    op0=ADD,
+                    op1=MULT,
                 )
 
-        zil, zc, zsc, ZT, O = {}, {}, {}, {}, {}
+        z_turned, z_words, z_codes, z_scales, out_sum = {}, {}, {}, {}, {}
 
-        def zint(b, engine):
-            z_il = zcp.tile([P, T, 4], BF16, name="z_il", align_bytes=64)
-            zil[b] = z_il
-            z_src = zr[b][:].rearrange("p j t -> p t j")
-            if engine == "V":
-                nc.vector.tensor_copy(out=z_il[:], in_=z_src)
-            else:
-                nc.scalar.copy(out=z_il[:], in_=z_src)
-
-        def zturn(b):
-            zt_ps = psum.tile([P, T, 4], BF16, name="zt_ps", tag="O")
+        def turn_z(b):
+            turned = psum.tile([P, T, 4], BF16, name="z_turned", tag="O")
             for c in range(2):
                 t = slice(c * P, (c + 1) * P)
                 nc.tensor.matmul(
-                    zt_ps[:, t, :].rearrange("p t j -> p j t"), lhsT=ident_b[:], rhs=zr[b][:, :, t], start=True, stop=True
-                )
-            ZT[b] = zt_ps
-
-        def zcopy(b):
-            z_il = zcp.tile([P, T, 4], BF16, name="z_il", align_bytes=64)
-            nc.scalar.copy(out=z_il[:].rearrange("p t j -> p (t j)"), in_=ZT[b][:].rearrange("p t j -> p (t j)"))
-            zil[b] = z_il
-
-        def zq(b):
-            z_q = zcp.tile([P, T], U32, name="z_q", align_bytes=64)
-            z_s = zcp.tile([P, T], U8, name="z_s", align_bytes=64)
-            nc.vector.quantize_mx(
-                out=z_q[:].bitcast(X4), scales=z_s[:], in_=zil[b][:].rearrange("p t j -> p (t j)")
-            )
-            zc[b], zsc[b] = z_q, z_s
-
-        def omm(b):
-            o_ps = psum.tile([P, 2, E], F32, name="o_ps", tag="O")
-            for c in range(2):
-                nc.tensor.matmul_mx(
-                    out=o_ps[:, c, :],
-                    lhsT=zc[b][:, c * P : (c + 1) * P].bitcast(X4),
-                    lhsT_scale=zsc[b][:, c * P : (c + 1) * P],
-                    rhs=w_q[:].bitcast(X4),
-                    rhs_scale=w_s[:],
+                    turned[:, t, :].rearrange("p t j -> p j t"),
+                    lhsT=ident_bf16[:],
+                    rhs=z_tile[b][:, :, t],
                     start=True,
                     stop=True,
                 )
-            O[b] = o_ps
+            z_turned[b] = turned
 
-        def ocopy(b):
-            o_sb = op.tile([P, 2, E], F32, name="o_sb", align_bytes=64)
-            nc.scalar.copy(out=o_sb[:], in_=O[b][:])
+        def fetch_z(b):
+            words = zq_pool.tile([P, T, 4], BF16, name="z_words", align_bytes=64)
+            if b == DIRECT:
+                nc.scalar.copy(out=words[:], in_=z_tile[b][:].rearrange("p j t -> p t j"))
+            else:
+                nc.scalar.copy(
+                    out=words[:].rearrange("p t j -> p (t j)"), in_=z_turned[b][:].rearrange("p t j -> p (t j)")
+                )
+            z_words[b] = words
+
+        def quantize_z(b):
+            codes = zq_pool.tile([P, T], U32, name="z_q", align_bytes=64)
+            scales = zq_pool.tile([P, T], U8, name="z_qs", align_bytes=64)
+            nc.vector.quantize_mx(
+                out=codes[:].bitcast(X4), scales=scales[:], in_=z_words[b][:].rearrange("p t j -> p (t j)")
+            )
+            z_codes[b], z_scales[b] = codes, scales
+
+        def project(b):
+            o_ps = psum.tile([P, 2, E], F32, name="o_ps", tag="O")
+            for c in range(2):
+                cols = slice(c * P, (c + 1) * P)
+                nc.tensor.matmul_mx(
+                    out=o_ps[:, c, :],
+                    lhsT=z_codes[b][:, cols].bitcast(X4),
+                    lhsT_scale=z_scales[b][:, cols],
+                    rhs=wo_codes[:].bitcast(X4),
+                    rhs_scale=wo_scales[:],
+                    start=True,
+                    stop=True,
+                )
+            out_sum[b] = o_ps
+
+        def store(b):
+            o_sb = out_pool.tile([P, 2, E], F32, name="o_sb", align_bytes=64)
+            nc.scalar.copy(out=o_sb[:], in_=out_sum[b][:])
             nc.sync.dma_start(out=out[b].rearrange("(p c) e -> p c e", c=2), in_=o_sb[:])
 
-        cf = const.tile([P, 12], F32, name="cf", align_bytes=64)
-        gc = const.tile([P, 8], F32, name="gc", align_bytes=64)
-        c_ps = psum.tile([P, P], BF16, name="c_ps", tag="O")
-        nc.vector.tensor_copy(out=ident_b[:], in_=ident[:])
-        widen(0, 1, "V")
-        widen(0, 2, "V")
-        widen(0, 3, "V")
-        widen(0, 0, "S")
-        m_turn(0)
-        xint(0)
-        nc.tensor.transpose(c_ps[:], rows[:], ident_b[:])
-        m_turn(1)
-        nc.vector.tensor_copy(out=cf[:], in_=c_ps[:, 0:12])
-        m_quant(0)
-        xq(0)
-        nc.vector.tensor_tensor(out=gc[:, 0:4], in0=cf[:, 0:4], in1=cf[:, 8:12], op=MULT)
-        nc.vector.tensor_tensor(out=gc[:, 4:8], in0=cf[:, 4:8], in1=cf[:, 8:12], op=MULT)
-        m_turn(2)
-        m_quant(1)
-        widen(1, 0, "V")
-        widen(1, 1, "V")
-        m_quant(2)
-        widen(1, 2, "V")
-        widen(1, 3, "V")
+        vec_cols = const.tile([P, 12], F32, name="vec_cols", align_bytes=64)
+        gain_coef = const.tile([P, 8], F32, name="gain_coef", align_bytes=64)
+        vec_ps = psum.tile([P, P], BF16, name="vec_ps", tag="O")
+        nc.vector.tensor_copy(out=ident_bf16[:], in_=ident_f32[:])
+        for t in (1, 2, 3):
+            widen("vector", 0, t)
+        widen("scalar", 0, 0)
+        turn_m(0)
+        interleave_x(0)
+        nc.tensor.transpose(vec_ps[:], vec_rows[:], ident_bf16[:])
+        turn_m(1)
+        nc.vector.tensor_copy(out=vec_cols[:], in_=vec_ps[:, 0:12])
+        quantize_m(0)
+        quantize_x(0)
+        nc.vector.tensor_tensor(out=gain_coef[:, 0:4], in0=vec_cols[:, 0:4], in1=vec_cols[:, 8:12], op=MULT)
+        nc.vector.tensor_tensor(out=gain_coef[:, 4:8], in0=vec_cols[:, 4:8], in1=vec_cols[:, 8:12], op=MULT)
+        turn_m(2)
+        quantize_m(1)
+        widen("vector", 1, 0)
+        widen("vector", 1, 1)
+        quantize_m(2)
+        widen("vector", 1, 2)
+        widen("vector", 1, 3)
 
-        total = 2 * NB
-        w_il = const.tile([P, E, 4], BF16, name="w_il", align_bytes=64)
-        w_q = const.tile([P, E], U32, name="w_q", align_bytes=64)
-        w_s = const.tile([P, E], U8, name="w_s", align_bytes=64)
+        wo_words = const.tile([P, E, 4], BF16, name="wo_words", align_bytes=64)
+        wo_codes = const.tile([P, E], U32, name="wo_q", align_bytes=64)
+        wo_scales = const.tile([P, E], U8, name="wo_qs", align_bytes=64)
 
-        def w_int():
-            nc.vector.tensor_copy(out=w_il[:], in_=w_raw[:].rearrange("p j e -> p e j"))
+        products(0)
+        third_order(0)
+        for t in (0, 1, 2):
+            widen("scalar", 2, t)
+        interleave_x(1)
+        products(1)
+        third_order(1)
+        widen("scalar", 2, 3)
+        for t in range(4):
+            widen("scalar", 3, t)
+        times_q(0)
+        quantize_x(1)
+        interleave_x(2)
 
-        def w_quant():
+        for n in range(STEPS):
+            even = n % 2 == 0
+            if n + 1 < STEPS:
+                times_q(n + 1)
+            times_p(n)
+
+            if n == 0:
+                nc.vector.tensor_copy(out=wo_words[:], in_=wo_rows[:].rearrange("p j e -> p e j"))
+            if n == 2:
+                nc.vector.quantize_mx(
+                    out=wo_codes[:].bitcast(X4), scales=wo_scales[:], in_=wo_words[:].rearrange("p e j -> p (e j)")
+                )
+            if not even and (n + 3) // 2 < NB:
+                quantize_x((n + 3) // 2)
+            if not even and (n + 5) // 2 < NB:
+                interleave_x((n + 5) // 2)
+            if even and n >= 4:
+                quantize_z((n - 4) // 2)
+
+            if n + 2 < STEPS:
+                products(n + 2)
+                third_order(n + 2)
+
+            if even and n >= 2:
+                fetch_z((n - 2) // 2)
+            if not even and n >= 5:
+                store((n - 5) // 2)
+            if n == 0:
+                widen("scalar", SINGLE, 0)
+            t = (n + 1) % 4
+            pair = (n + 9 - t) // 2
+            if pair < NB:
+                widen("scalar", pair, t)
+
+            if not even and n // 2 not in (DIRECT, LAST):
+                turn_z(n // 2)
+            if even and n >= 4:
+                project((n - 4) // 2)
+
+        quantize_z(LAST - 1)
+        project(LAST - 1)
+        store(LAST - 1)
+        half_words = []
+        for c in range(2):
+            words = zq_pool.tile([P, P, 4], BF16, name="half_words%d" % c, align_bytes=64)
+            nc.vector.tensor_copy(
+                out=words[:], in_=z_tile[LAST][:, :, c * P : (c + 1) * P].rearrange("p j t -> p t j")
+            )
+            half_words.append(words)
+        for c in range(2):
+            codes = zq_pool.tile([P, P], U32, name="half_q%d" % c, align_bytes=64)
+            scales = zq_pool.tile([P, P], U8, name="half_qs%d" % c, align_bytes=64)
             nc.vector.quantize_mx(
-                out=w_q[:].bitcast(X4), scales=w_s[:], in_=w_il[:].rearrange("p e j -> p (e j)")
+                out=codes[:].bitcast(X4), scales=scales[:], in_=half_words[c][:].rearrange("p t j -> p (t j)")
             )
-
-        def wid(b, *ts):
-            for t in ts:
-                widen(b, t, "S")
-
-        before = [[] for n in range(total + 12)]
-        leading = [[] for n in range(total + 12)]
-        after = [[] for n in range(total + 12)]
-
-        def put(where, n, *call):
-            where[n].append(call)
-
-        put(before, 0, w_int)
-        put(before, 2, w_quant)
-        for b in range(2, NB):
-            if b > 2:
-                put(before, 2 * b - 5, xint, b)
-            put(before, 2 * b - 3, xq, b)
-        for b in range(4, NB, 2):
-            for t in range(4):
-                put(after, max(0, 2 * b - 9 + t - AHEAD), wid, b, t)
-        for b in range(NB - 1):
-            how = ZHOW.get(b, "P")
-            if how == "P":
-                put(after, 2 * b + 1, zturn, b)
-                put(leading, 2 * b + 2, zcopy, b)
-            elif how == "S":
-                put(leading, 2 * b + 2, zint, b, "S")
-            else:
-                put(before, 2 * b + 3, zint, b, "V")
-            put(before, 2 * b + 4, zq, b)
-            put(after, 2 * b + 4, omm, b)
-            put(leading, 2 * b + 5, ocopy, b)
-        mm(0)
-        h_of(0)
-        wid(2, 0, 1, 2)
-        xint(1)
-        mm(1)
-        h_of(1)
-        wid(2, 3)
-        wid(3, 0, 1, 2, 3)
-        first(0)
-        xq(1)
-        xint(2)
-        for n in range(total):
-            if n + 1 < total:
-                first(n + 1)
-            second(n)
-            for fn, *args in before[n]:
-                fn(*args)
-            if n + 2 < total:
-                mm(n + 2)
-                h_of(n + 2)
-            for fn, *args in leading[n] + after[n]:
-                fn(*args)
-        for n in range(total, total + 12):
-            for fn, *args in before[n] + leading[n] + after[n]:
-                fn(*args)
-        b = NB - 1
-        zl = []
-        for c in range(2):
-            z_il = zcp.tile([P, P, 4], BF16, name="z_il%d" % c, align_bytes=64)
-            z_src = zr[b][:, :, c * P : (c + 1) * P].rearrange("p j t -> p t j")
-            nc.vector.tensor_copy(out=z_il[:], in_=z_src)
-            zl.append(z_il)
-        for c in range(2):
-            z_q = zcp.tile([P, P], U32, name="z_q%d" % c, align_bytes=64)
-            z_s = zcp.tile([P, P], U8, name="z_s%d" % c, align_bytes=64)
-            nc.vector.quantize_mx(out=z_q[:].bitcast(X4), scales=z_s[:], in_=zl[c][:].rearrange("p t j -> p (t j)"))
-            o_ps = psum.tile([P, E], F32, name="o_ps", tag="O")
+            half_ps = psum.tile([P, E], F32, name="half_ps", tag="O")
             nc.tensor.matmul_mx(
-                out=o_ps[:], lhsT=z_q[:].bitcast(X4), lhsT_scale=z_s[:], rhs=w_q[:].bitcast(X4), rhs_scale=w_s[:],
-                start=True, stop=True,
+                out=half_ps[:],
+                lhsT=codes[:].bitcast(X4),
+                lhsT_scale=scales[:],
+                rhs=wo_codes[:].bitcast(X4),
+                rhs_scale=wo_scales[:],
+                start=True,
+                stop=True,
             )
-            o_sb = op.tile([P, E], F32, name="o_sb%d" % c, align_bytes=64)
+            half_sb = out_pool.tile([P, E], F32, name="half_sb%d" % c, align_bytes=64)
             if c == 0:
-                nc.scalar.copy(out=o_sb[:], in_=o_ps[:])
+                nc.scalar.copy(out=half_sb[:], in_=half_ps[:])
             else:
-                nc.vector.tensor_copy(out=o_sb[:], in_=o_ps[:])
-            nc.sync.dma_start(out=out[b].rearrange("(p c) e -> p c e", c=2)[:, c, :], in_=o_sb[:])
+                nc.vector.tensor_copy(out=half_sb[:], in_=half_ps[:])
+            nc.sync.dma_start(out=out[LAST].rearrange("(p c) e -> p c e", c=2)[:, c, :], in_=half_sb[:])

from contextlib import ExitStack

import concourse.mybir as mybir
from concourse.masks import make_identity

NB, S, D, T, E = 16, 512, 512, 256, 256
P = 128
FLOPS = NB * (2 * 3 * T * S * D + 2 * T * D * E)

F32 = mybir.dt.float32
BF16 = mybir.dt.bfloat16
U32 = mybir.dt.uint32
U8 = mybir.dt.uint8
FP8 = mybir.dt.float8_e4m3fn
X4 = mybir.dt.float8_e4m3fn_x4
COPY = mybir.ActivationFunctionType.Copy
IDENTITY = mybir.ActivationFunctionType.Identity
ADD = mybir.AluOpType.add
MULT = mybir.AluOpType.mult

STEPS = 2 * NB
SINGLE = 4
LAST = NB - 1
DIRECT = NB - 3


def tile_volterrathirdordermixer_t_kernel(tc, x_bytes, x_scale, mp, mq, mr, coef, gain, wo, out):
    nc = tc.nc
    with ExitStack() as ctx:
        const = ctx.enter_context(tc.tile_pool(name="const", bufs=1))
        bytes_pool = ctx.enter_context(tc.tile_pool(name="bytes_pool", bufs=8))
        wide_pool = ctx.enter_context(tc.tile_pool(name="wide_pool", bufs=3))
        x_pool = ctx.enter_context(tc.tile_pool(name="x_pool", bufs=3))
        xq_pool = ctx.enter_context(tc.tile_pool(name="xq_pool", bufs=5))
        poly = ctx.enter_context(tc.tile_pool(name="poly", bufs=3))
        z_pool = ctx.enter_context(tc.tile_pool(name="z_pool", bufs=3))
        zq_pool = ctx.enter_context(tc.tile_pool(name="zq_pool", bufs=4))
        out_pool = ctx.enter_context(tc.tile_pool(name="out_pool", bufs=4))
        psum = ctx.enter_context(tc.psum_pool(name="psum", bufs=2))
        ctx.enter_context(tc.manual_schedule())

        x_raw = {}

        def load_x(b, width):
            codes = bytes_pool.tile([P, 4, width, D], U8, name="codes%d" % width, align_bytes=64)
            for k in range(width):
                nc.sync.dma_start(out=codes[:, :, k, :], in_=x_bytes[b + k].rearrange("(p t) d -> p t d", t=4))
            x_raw[b] = codes

        load_x(0, 1)
        scale = const.tile([P, 4], F32, name="scale", align_bytes=64)
        nc.sync.dma_start(out=scale[:], in_=x_scale.rearrange("o (p t) z -> p (o t z)", t=4))

        vec_rows = const.tile([P, P], BF16, name="vec_rows", align_bytes=64)
        first_act = const.tile([P, 1], F32, name="first_act")
        nc.vector.memset(vec_rows[:], 0.0)
        nc.vector.memset(first_act[:], 0.0)
        for v, vec in enumerate((coef[0], coef[1], gain)):
            nc.sync.dma_start(
                out=vec_rows[4 * v : 4 * v + 4, :].rearrange("p (g i) -> p g i", i=8),
                in_=vec.rearrange("(g j i) -> j g i", j=4, i=8),
            )
        m_raw = []
        for i, m in enumerate((mr, mq, mp)):
            m_rows = const.tile([P, 2, S], BF16, name="m_rows%d" % i, align_bytes=64)
            nc.sync.dma_start(out=m_rows[:], in_=m.rearrange("(p c) k -> p c k", c=2))
            m_raw.append(m_rows)
        for b in range(1, SINGLE):
            load_x(b, 1)

        nc.scalar.activation(out=first_act[:], in_=first_act[:], func=IDENTITY)
        ident_f32 = const.tile([P, P], F32, name="ident_f32", align_bytes=64)
        make_identity(nc, ident_f32[:])
        ident_bf16 = const.tile([P, P], BF16, name="ident_bf16", align_bytes=64)

        wo_rows = const.tile([P, 4, E], BF16, name="wo_rows", align_bytes=64)
        for g in range(16):
            nc.sync.dma_start(
                out=wo_rows[8 * g : 8 * g + 8, :, :],
                in_=wo[32 * g : 32 * g + 32, :].rearrange("(j i) e -> i j e", i=8),
            )
        for b in range(SINGLE, NB, 2):
            load_x(b, 2)

        x_wide, x_rows, x_words, x_codes, x_scales = {}, {}, {}, {}, {}

        def widen(engine, b, t):
            width = 1 if b < SINGLE else 2
            if b not in x_wide:
                wide = wide_pool.tile([P, 4, width, D], BF16, name="wide%d" % width, align_bytes=64)
                x_wide[b] = wide
                for k in range(width):
                    x_rows[b + k] = wide[:, :, k, :]
            dst = x_wide[b][:, t, :, :].rearrange("p b d -> p (b d)")
            src = x_raw[b][:, t, :, :].rearrange("p b d -> p (b d)").bitcast(FP8)
            if engine == "scalar":
                nc.scalar.activation(out=dst, in_=src, func=COPY, scale=scale[:, t : t + 1])
            else:
                nc.vector.tensor_scalar(out=dst, in0=src, scalar1=scale[:, t : t + 1], scalar2=None, op0=MULT)

        def interleave_x(b):
            words = x_pool.tile([P, 4 * D], BF16, name="words", align_bytes=64)
            nc.vector.tensor_copy(
                out=words[:].rearrange("p (j g i t) -> p g j t i", j=4, g=16, i=8, t=4),
                in_=x_rows[b].rearrange("p t (g j i) -> p g j t i", g=16, j=4, i=8),
            )
            x_words[b] = words

        def quantize_x(b):
            codes = xq_pool.tile([P, D], U32, name="x_q", align_bytes=64)
            scales = xq_pool.tile([P, D], U8, name="x_qs", align_bytes=64)
            nc.vector.quantize_mx(out=codes[:].bitcast(X4), scales=scales[:], in_=x_words[b][:])
            x_codes[b], x_scales[b] = codes, scales

        m_words, m_codes, m_scales = [], [], []

        def turn_m(i):
            turned = psum.tile([P, 2, 2, P], F32, name="turned", tag="RQP"[i])
            for c in range(2):
                words = m_raw[i][:, c, :].bitcast(F32)
                for u in range(2):
                    nc.tensor.transpose(turned[:, c, u, :], words[:, u : S // 2 : 2], ident_f32[:])
            grouped = const.tile([P, T, 4], BF16, name="m_words%d" % i, align_bytes=64)
            dst = grouped[:].rearrange("p n t -> p (n t)").bitcast(F32)
            nc.scalar.copy(
                out=dst.rearrange("p (c n u) -> p c n u", c=2, u=2), in_=turned[:].rearrange("p c u n -> p c n u")
            )
            m_words.append(grouped)

        def quantize_m(i):
            codes = const.tile([P, T], U32, name="m_q%d" % i, align_bytes=64)
            scales = const.tile([P, T], U8, name="m_qs%d" % i, align_bytes=64)
            nc.vector.quantize_mx(
                out=codes[:].bitcast(X4), scales=scales[:], in_=m_words[i][:].rearrange("p n t -> p (n t)")
            )
            m_codes.append(codes)
            m_scales.append(scales)

        r_sum, q_sum, p_sum, h_val, u_val, z_tile = {}, {}, {}, {}, {}, {}

        def products(n):
            b, j0 = n // 2, 2 * (n % 2)
            r_ps = psum.tile([P, 2, T], F32, name="r_ps", tag="R")
            q_ps = psum.tile([P, 2, T], F32, name="q_ps", tag="Q")
            p_ps = psum.tile([P, 2, T], F32, name="p_ps", tag="P")
            for i, ps in enumerate((r_ps, q_ps, p_ps)):
                for k in range(2):
                    cols = slice((j0 + k) * P, (j0 + k + 1) * P)
                    nc.tensor.matmul_mx(
                        out=ps[:, k, :],
                        lhsT=x_codes[b][:, cols].bitcast(X4),
                        lhsT_scale=x_scales[b][:, cols],
                        rhs=m_codes[i][:].bitcast(X4),
                        rhs_scale=m_scales[i][:],
                        start=True,
                        stop=True,
                    )
            r_sum[n], q_sum[n], p_sum[n] = r_ps, q_ps, p_ps

        def third_order(n):
            h = poly.tile([P, 2, T], F32, name="h", align_bytes=64)
            for k in range(2):
                j = 2 * (n % 2) + k
                nc.scalar.activation(
                    out=h[:, k, :],
                    in_=r_sum[n][:, k, :],
                    func=IDENTITY,
                    bias=gain_coef[:, j : j + 1],
                    scale=gain_coef[:, 4 + j : 5 + j],
                )
            h_val[n] = h

        def times_q(n):
            u = poly.tile([P, 2, T], F32, name="u", align_bytes=64)
            nc.vector.tensor_tensor(out=u[:], in0=h_val[n][:], in1=q_sum[n][:], op=MULT)
            u_val[n] = u

        def times_p(n):
            b = n // 2
            if n % 2 == 0:
                z_rows = z_pool.tile([P, 4, T], BF16, name="z_rows", align_bytes=64)
                z_tile[b] = z_rows
            for k in range(2):
                j = 2 * (n % 2) + k
                nc.vector.scalar_tensor_tensor(
                    out=z_tile[b][:, j, :],
                    in0=u_val[n][:, k, :],
                    scalar=vec_cols[:, 8 + j : 9 + j],
                    in1=p_sum[n][:, k, :],
                    op0=ADD,
                    op1=MULT,
                )

        z_turned, z_words, z_codes, z_scales, out_sum = {}, {}, {}, {}, {}

        def turn_z(b):
            turned = psum.tile([P, T, 4], BF16, name="z_turned", tag="O")
            for c in range(2):
                t = slice(c * P, (c + 1) * P)
                nc.tensor.matmul(
                    turned[:, t, :].rearrange("p t j -> p j t"),
                    lhsT=ident_bf16[:],
                    rhs=z_tile[b][:, :, t],
                    start=True,
                    stop=True,
                )
            z_turned[b] = turned

        def fetch_z(b):
            words = zq_pool.tile([P, T, 4], BF16, name="z_words", align_bytes=64)
            if b == DIRECT:
                nc.scalar.copy(out=words[:], in_=z_tile[b][:].rearrange("p j t -> p t j"))
            else:
                nc.scalar.copy(
                    out=words[:].rearrange("p t j -> p (t j)"), in_=z_turned[b][:].rearrange("p t j -> p (t j)")
                )
            z_words[b] = words

        def quantize_z(b):
            codes = zq_pool.tile([P, T], U32, name="z_q", align_bytes=64)
            scales = zq_pool.tile([P, T], U8, name="z_qs", align_bytes=64)
            nc.vector.quantize_mx(
                out=codes[:].bitcast(X4), scales=scales[:], in_=z_words[b][:].rearrange("p t j -> p (t j)")
            )
            z_codes[b], z_scales[b] = codes, scales

        def project(b):
            o_ps = psum.tile([P, 2, E], F32, name="o_ps", tag="O")
            for c in range(2):
                cols = slice(c * P, (c + 1) * P)
                nc.tensor.matmul_mx(
                    out=o_ps[:, c, :],
                    lhsT=z_codes[b][:, cols].bitcast(X4),
                    lhsT_scale=z_scales[b][:, cols],
                    rhs=wo_codes[:].bitcast(X4),
                    rhs_scale=wo_scales[:],
                    start=True,
                    stop=True,
                )
            out_sum[b] = o_ps

        def store(b):
            o_sb = out_pool.tile([P, 2, E], F32, name="o_sb", align_bytes=64)
            nc.scalar.copy(out=o_sb[:], in_=out_sum[b][:])
            nc.sync.dma_start(out=out[b].rearrange("(p c) e -> p c e", c=2), in_=o_sb[:])

        vec_cols = const.tile([P, 12], F32, name="vec_cols", align_bytes=64)
        gain_coef = const.tile([P, 8], F32, name="gain_coef", align_bytes=64)
        vec_ps = psum.tile([P, P], BF16, name="vec_ps", tag="O")
        nc.vector.tensor_copy(out=ident_bf16[:], in_=ident_f32[:])
        for t in (1, 2, 3):
            widen("vector", 0, t)
        widen("scalar", 0, 0)
        turn_m(0)
        interleave_x(0)
        nc.tensor.transpose(vec_ps[:], vec_rows[:], ident_bf16[:])
        turn_m(1)
        nc.vector.tensor_copy(out=vec_cols[:], in_=vec_ps[:, 0:12])
        quantize_m(0)
        quantize_x(0)
        nc.vector.tensor_tensor(out=gain_coef[:, 0:4], in0=vec_cols[:, 0:4], in1=vec_cols[:, 8:12], op=MULT)
        nc.vector.tensor_tensor(out=gain_coef[:, 4:8], in0=vec_cols[:, 4:8], in1=vec_cols[:, 8:12], op=MULT)
        turn_m(2)
        quantize_m(1)
        widen("vector", 1, 0)
        widen("vector", 1, 1)
        quantize_m(2)
        widen("vector", 1, 2)
        widen("vector", 1, 3)

        wo_words = const.tile([P, E, 4], BF16, name="wo_words", align_bytes=64)
        wo_codes = const.tile([P, E], U32, name="wo_q", align_bytes=64)
        wo_scales = const.tile([P, E], U8, name="wo_qs", align_bytes=64)

        products(0)
        third_order(0)
        for t in (0, 1, 2):
            widen("scalar", 2, t)
        interleave_x(1)
        products(1)
        third_order(1)
        widen("scalar", 2, 3)
        for t in range(4):
            widen("scalar", 3, t)
        times_q(0)
        quantize_x(1)
        interleave_x(2)

        for n in range(STEPS):
            even = n % 2 == 0
            if n + 1 < STEPS:
                times_q(n + 1)
            times_p(n)

            if n == 0:
                nc.vector.tensor_copy(out=wo_words[:], in_=wo_rows[:].rearrange("p j e -> p e j"))
            if n == 2:
                nc.vector.quantize_mx(
                    out=wo_codes[:].bitcast(X4), scales=wo_scales[:], in_=wo_words[:].rearrange("p e j -> p (e j)")
                )
            if not even and (n + 3) // 2 < NB:
                quantize_x((n + 3) // 2)
            if not even and (n + 5) // 2 < NB:
                interleave_x((n + 5) // 2)
            if even and n >= 4:
                quantize_z((n - 4) // 2)

            if n + 2 < STEPS:
                products(n + 2)
                third_order(n + 2)

            if even and n >= 2:
                fetch_z((n - 2) // 2)
            if not even and n >= 5:
                store((n - 5) // 2)
            if n == 0:
                widen("scalar", SINGLE, 0)
            t = (n + 1) % 4
            pair = (n + 9 - t) // 2
            if pair < NB:
                widen("scalar", pair, t)

            if not even and n // 2 not in (DIRECT, LAST):
                turn_z(n // 2)
            if even and n >= 4:
                project((n - 4) // 2)

        quantize_z(LAST - 1)
        project(LAST - 1)
        store(LAST - 1)
        half_words = []
        for c in range(2):
            words = zq_pool.tile([P, P, 4], BF16, name="half_words%d" % c, align_bytes=64)
            nc.vector.tensor_copy(
                out=words[:], in_=z_tile[LAST][:, :, c * P : (c + 1) * P].rearrange("p j t -> p t j")
            )
            half_words.append(words)
        for c in range(2):
            codes = zq_pool.tile([P, P], U32, name="half_q%d" % c, align_bytes=64)
            scales = zq_pool.tile([P, P], U8, name="half_qs%d" % c, align_bytes=64)
            nc.vector.quantize_mx(
                out=codes[:].bitcast(X4), scales=scales[:], in_=half_words[c][:].rearrange("p t j -> p (t j)")
            )
            half_ps = psum.tile([P, E], F32, name="half_ps", tag="O")
            nc.tensor.matmul_mx(
                out=half_ps[:],
                lhsT=codes[:].bitcast(X4),
                lhsT_scale=scales[:],
                rhs=wo_codes[:].bitcast(X4),
                rhs_scale=wo_scales[:],
                start=True,
                stop=True,
            )
            half_sb = out_pool.tile([P, E], F32, name="half_sb%d" % c, align_bytes=64)
            if c == 0:
                nc.scalar.copy(out=half_sb[:], in_=half_ps[:])
            else:
                nc.vector.tensor_copy(out=half_sb[:], in_=half_ps[:])
            nc.sync.dma_start(out=out[LAST].rearrange("(p c) e -> p c e", c=2)[:, c, :], in_=half_sb[:])
